import numpy as np
import ml_dtypes


def mxq(x, axis, fmt="e4m3"):
    dtype, down = {"e4m3": (ml_dtypes.float8_e4m3fn, 7), "e5m2": (ml_dtypes.float8_e5m2, 14)}[fmt]
    v = np.moveaxis(np.asarray(x, np.float32).astype(ml_dtypes.bfloat16).astype(np.float64), axis, -1)
    blocks = v.reshape(v.shape[:-1] + (-1, 32))
    amax = np.abs(blocks).max(-1, keepdims=True)
    byte = np.maximum(np.where(amax > 0, np.frexp(amax)[1] - 1 + 127, 0) - down, 1)
    scale = np.exp2(byte - 127.0)
    codes = (blocks / scale).astype(np.float32).astype(dtype).astype(np.float64)
    return np.moveaxis((codes * scale).reshape(v.shape), -1, axis)


WIDE = False


def mx_kscale(k):
    if not WIDE:
        return np.ones(k)
    levels = np.array([10, -10, 5, -5, 0])
    if k % 512:
        return np.exp2(np.random.permutation(np.resize(levels, k // 32))).repeat(32)
    a = np.empty((k // 512, 16))
    for p in range(k // 512):
        a[p, :8] = np.random.permutation(np.resize(levels, 8))
        for g in range(8):
            far = levels[np.abs(levels - a[p, g]) >= 10]
            a[p, g + 8] = far[np.random.randint(len(far))]
    return np.exp2(a.ravel()).repeat(32)


def f64(x):
    return np.asarray(x).astype(np.float64)


def striped(idx):
    return np.tile(idx.reshape(-1, 16).T, (8, 1)).astype(np.uint16)


def unstriped(offs):
    return offs[:16].T.reshape(-1).astype(np.int64)


E2M1 = np.array([0.0, 0.5, 1.0, 1.5, 2.0, 3.0, 4.0, 6.0, -0.0, -0.5, -1.0, -1.5, -2.0, -3.0, -4.0, -6.0])


def pack_weight(w, fmt):
    k, n = w.shape
    w = f64(np.asarray(w, np.float32).astype(ml_dtypes.bfloat16)).reshape(k // 32, 32, n)
    amax = np.abs(w).max(1)
    if fmt == "e4m3":
        byte = np.frexp(amax)[1] - 1 + 127 - 7
    else:
        mant, ex = np.frexp(amax / 6.0)
        byte = np.where(mant > 0.5, ex, ex - 1) + 127
    byte = np.clip(np.where(amax > 0, byte, 1), 1, 254)
    scaled = (w * np.exp2(127.0 - byte)[:, None, :]).reshape(k, n).astype(np.float32)
    by_word = np.ascontiguousarray(scaled.reshape(k // 512, 128, 4, n).transpose(0, 1, 3, 2))
    if fmt == "e4m3":
        words = by_word.astype(ml_dtypes.float8_e4m3fn).view(np.uint8)
    else:
        c = by_word.astype(ml_dtypes.float4_e2m1fn).view(np.uint8) & 0xF
        words = (c[..., 0::2] | (c[..., 1::2] << 4)).reshape(k // 512, 128, 2 * n)
    return np.ascontiguousarray(words), np.ascontiguousarray(byte.astype(np.uint8).reshape(k // 512, 16, n))


def unpack_weight(words, scales, fmt):
    g, _, n = scales.shape
    words = np.ascontiguousarray(words).reshape(g, 128, n, -1)
    if fmt == "e4m3":
        vals = words.view(ml_dtypes.float8_e4m3fn).astype(np.float64)
    else:
        nib = np.empty((g, 128, n, 4), np.uint8)
        nib[..., 0::2] = words & 0xF
        nib[..., 1::2] = words >> 4
        vals = E2M1[nib]
    vals = vals * np.repeat(np.exp2(scales.astype(np.float64) - 127.0), 8, axis=1)[..., None]
    return vals.transpose(0, 1, 3, 2).reshape(g * 512, n)


def gelu(v):
    return 0.5 * v * (1.0 + np.tanh(np.sqrt(2.0 / np.pi) * (v + 0.044715 * v**3)))


def striped8(idx):
    return np.concatenate([v.reshape(-1, 16).T for v in idx]).astype(np.uint16)


def unstriped8(offs):
    return np.stack([offs[16 * g:16 * g + 16].T.reshape(-1) for g in range(8)]).astype(np.int64)


def runs(v, idx8):
    k = np.arange(v.shape[0])
    return v[k[:, None], idx8[k % 512 // 64]]


K, K2, H, N, T, T2, S = 1024, 512, 1024, 512, 2048, 1024, 512

def setup_inputs():
    n = np.random.standard_normal
    s = mx_kscale(K)[:, None]
    s2 = mx_kscale(K2)[:, None]
    u = mx_kscale(H)[:, None]
    tab_words, tab_scales = pack_weight(n((K, T)) * s, "e4m3")
    tab2_words, tab2_scales = pack_weight(n((K2, T2)) * s2, "e4m3")
    wsub_words, wsub_scales = pack_weight(n((K, H)) / np.sqrt(K) / s, "e2m1")
    winh = (n((K2, H)) / np.sqrt(K2) / s2).astype(np.float32)
    vmax = (2.0 * np.exp(0.3 * n(H)) * u[:, 0]).astype(np.float32)
    wread_words, wread_scales = pack_weight(n((H, N)) / np.sqrt(H) / u, "e4m3")
    return {"tab_words": tab_words, "tab_scales": tab_scales,
            "offs": striped8(np.stack([np.random.permutation(T)[:S] for _ in range(8)])),
            "tab2_words": tab2_words, "tab2_scales": tab2_scales,
            "offs2": striped(np.random.permutation(T2)[:S]),
            "wsub_words": wsub_words, "wsub_scales": wsub_scales,
            "winh": winh, "vmax": vmax,
            "wread_words": wread_words, "wread_scales": wread_scales}

def reference(tab_words, tab_scales, offs, tab2_words, tab2_scales, offs2,
              wsub_words, wsub_scales, winh, vmax, wread_words, wread_scales):
    v = runs(unpack_weight(tab_words, tab_scales, "e4m3"), unstriped8(offs))
    v2 = unpack_weight(tab2_words, tab2_scales, "e4m3")[:, unstriped(offs2)]
    a = unpack_weight(wsub_words, wsub_scales, "e2m1").T @ v
    b = mxq(f64(winh), 0, "e4m3").T @ v2
    sub = a * a
    inh = b * b
    h = f64(vmax)[:, None] * (sub / (1.0 + sub + inh))
    wread = unpack_weight(wread_words, wread_scales, "e4m3")
    return wread.T @ mxq(h, 0, "e4m3")

@@ -1,0 +1,223 @@
+from contextlib import ExitStack
+
+import concourse.mybir as mybir
+
+K, K2, H, N, T, T2, S = 1024, 512, 1024, 512, 2048, 1024, 512
+FLOPS = 2 * S * (K * H + K2 * H + H * N)
+
+F32 = mybir.dt.float32
+BF16 = mybir.dt.bfloat16
+I32 = mybir.dt.int32
+U32 = mybir.dt.uint32
+U16 = mybir.dt.uint16
+U8 = mybir.dt.uint8
+FP8X4 = mybir.dt.float8_e4m3fn_x4
+FP4X4 = mybir.dt.float4_e2m1fn_x4
+ACT = mybir.ActivationFunctionType
+ALU = mybir.AluOpType
+
+P = 128
+PACK = 4
+PASS = P * PACK
+QUADS = 4
+SHIFT = 14
+HALF = S // 2
+
+
+def tile_list_competitive_inhibitor_assay_kernel(
+    tc, tab_words, tab_scales, offs, tab2_words, tab2_scales, offs2,
+    wsub_words, wsub_scales, winh, vmax, wread_words, wread_scales, out,
+):
+    nc = tc.nc
+    with ExitStack() as ctx:
+        keep = ctx.enter_context(tc.tile_pool(name="keep", bufs=1))
+        ring = ctx.enter_context(tc.tile_pool(name="ring", bufs=3))
+        psum_a = ctx.enter_context(tc.psum_pool(name="psum_a", bufs=3))
+        psum_b = ctx.enter_context(tc.psum_pool(name="psum_b", bufs=3))
+        psum_o = ctx.enter_context(tc.psum_pool(name="psum_o", bufs=2))
+
+        def held(shape, dtype, name):
+            return keep.tile(shape, dtype, name=name, align_bytes=64)
+
+        lists = keep.tile([P, S // 16], U16, name="lists")
+        list2 = keep.tile([P, S // 16], U16, name="list2")
+        nc.sync.dma_start(lists[:], offs)
+        nc.sync.dma_start(list2[:], offs2)
+
+        one = held([P, 1], F32, "one")
+        warm = keep.tile([P, 1], F32, name="warm", tag="table0", align_bytes=64)
+
+        tab_sc = held([P, 2 * T], U8, "tab_sc")
+        tab2_sc = held([P, T2], U8, "tab2_sc")
+        wsub_sc = held([P, 2, H], U8, "wsub_sc")
+        wread_sc = held([P, 2, N], U8, "wread_sc")
+        v_sc = held([P, 2 * S], U8, "v_sc")
+        nc.vector.memset(tab_sc[:].bitcast(I32), 0)
+        nc.vector.memset(one[:], 1.0)
+        nc.scalar.activation(warm[:], one[:], ACT.Abs_reciprocal_sqrt, bias=one[:])
+        nc.vector.memset(wsub_sc[:].bitcast(I32), 0)
+        nc.vector.memset(tab2_sc[:].bitcast(I32), 0)
+        nc.vector.memset(v_sc[:].bitcast(I32), 0)
+        nc.vector.memset(wread_sc[:].bitcast(I32), 0)
+
+        def load_scale_rows(queue, dst, src, first):
+            for d in range(QUADS):
+                queue.dma_start(dst[32 * d + first : 32 * d + first + 4],
+                                src[:, 4 * d : 4 * d + 4, :].rearrange("a q c -> q a c"))
+
+
+        def words(src):
+            return src.rearrange("p t i -> p (t i)").bitcast(I32)
+
+        winh_rows = winh.rearrange("(p j) c -> p j c", j=PACK)
+        rate = held([P, 2, PACK], F32, "rate")
+        winh_raw, wsub_raw = [], []
+
+        def shared(shape, dtype, name, tag):
+            return keep.tile(shape, dtype, name=name, tag=tag, align_bytes=64)
+
+        def load_wsub(a):
+            raw = shared([P, 2, 2 * PASS], U8, "wsub_raw%d" % a, "wsub_raw")
+            nc.sync.dma_start(raw[:].bitcast(I32),
+                              wsub_words.bitcast(I32)[:, :, a * PASS // 2 : (a + 1) * PASS // 2].rearrange("g p c -> p g c"))
+            wsub_raw.append(raw)
+
+        nc.sync.dma_start(rate[:], vmax.rearrange("(a p t) -> p a t", a=2, t=PACK))
+        load_wsub(0)
+        tab2_w = shared([P, T2], I32, "tab2_w", "table1")
+        nc.sync.dma_start(tab2_w[:], words(tab2_words[0]))
+        winh_raw.append([held([P, PACK, PASS // 2], F32, "winh_raw%d" % u)[:] for u in range(2)])
+        for u in range(2):
+            nc.sync.dma_start(winh_raw[0][u], winh_rows[:, :, u * PASS // 2 : (u + 1) * PASS // 2])
+        load_scale_rows(nc.sync, tab_sc[:].bitcast(I32).rearrange("p (a c) -> p a c", a=2),
+                        tab_scales.bitcast(I32), SHIFT)
+        tab_w = [shared([P, T], I32, "tab_w0", "table0")]
+        nc.sync.dma_start(tab_w[0][:], words(tab_words[0]))
+        load_scale_rows(nc.sync, tab2_sc[:].bitcast(I32).rearrange("p (a c) -> p a c", a=1),
+                        tab2_scales.bitcast(I32), 0)
+
+        v2_w = held([P, S], U32, "v2_w")
+        v2_sc = held([P, S], U8, "v2_sc")
+        v_w = [held([P, S], U32, "v_w%d" % g) for g in range(2)]
+        tab_sc1 = held([P, T], U8, "tab_sc1")
+        picked_sc = held([P, 2 * S], U8, "picked_sc")
+        nc.vector.tensor_copy(v2_w[:], tab2_w[:].bitcast(U32).indirect(list2[:]))
+        tab_w.append(shared([P, T], I32, "tab_w1", "table1"))
+        nc.sync.dma_start(tab_w[1][:], words(tab_words[1]))
+        load_scale_rows(nc.sync, wsub_sc[:].bitcast(I32), wsub_scales.bitcast(I32), 0)
+        nc.vector.tensor_copy(tab_sc1[:].bitcast(I32), tab_sc[:].bitcast(I32)[:, T // 4 :])
+        nc.vector.tensor_copy(picked_sc[:, :S], tab_sc[:].indirect(lists[:]))
+        nc.vector.tensor_copy(picked_sc[:, S:], tab_sc1[:].indirect(lists[:]))
+        rows = 112
+        nc.sync.dma_start(v_sc[:rows].bitcast(I32), picked_sc[SHIFT : SHIFT + rows].bitcast(I32))
+        nc.vector.tensor_copy(v2_sc[:], tab2_sc[:].indirect(list2[:]))
+
+        winh_w, winh_sc, wsub_w, wsub_s = [], [], [], []
+
+        def prepare_winh(a):
+            grouped = held([P, PACK, P, PACK], BF16, "winh_bf%d" % a)
+            for u in range(2):
+                nc.scalar.activation(
+                    grouped[:, :, u * P // 2 : (u + 1) * P // 2, :].rearrange("p t m j -> p m j t"),
+                    winh_raw[a][u].rearrange("p j (m t) -> p m j t", t=PACK), ACT.Copy)
+            codes = held([P, PASS], U32, "winh_w%d" % a)
+            scales = held([P, PASS], U8, "winh_sc%d" % a)
+            nc.vector.quantize_mx(out=codes[:].bitcast(FP8X4), scales=scales[:],
+                                  in_=grouped[:].rearrange("p t m j -> p (t m j)"))
+            winh_w.append(codes)
+            winh_sc.append(scales)
+
+        def prepare_wsub(a):
+            codes = held([P, 2, 2 * PASS], U8, "wsub_w%d" % a)
+            scales = held([P, 2, PASS], U8, "wsub_s%d" % a)
+            nc.vector.tensor_copy(codes[:].bitcast(U16).rearrange("p g (t m) -> p g m t", t=PACK),
+                                  wsub_raw[a][:].bitcast(U16).rearrange("p g (m t) -> p g m t", t=PACK))
+            nc.vector.tensor_copy(scales[:].rearrange("p g (t m) -> p g m t", t=PACK),
+                                  wsub_sc[:, :, a * PASS : (a + 1) * PASS].rearrange("p g (m t) -> p g m t", t=PACK))
+            wsub_w.append(codes)
+            wsub_s.append(scales)
+
+        inh = [held([P, PACK, S], F32, "inh%d" % a) for a in range(2)]
+        sub = [held([P, PACK, S], F32, "sub%d" % a) for a in range(2)]
+        root = [held([P, PACK, S], F32, "root%d" % a) for a in range(2)]
+        part = [held([P, PACK, S], F32, "part%d" % a) for a in range(2)]
+        h_w = [[held([P, HALF], U32, "h_w%d%d" % (a, u)) for u in range(2)] for a in range(2)]
+        h_sc = [[held([P, HALF], U8, "h_sc%d%d" % (a, u)) for u in range(2)] for a in range(2)]
+
+        def inhibitor(a, t):
+            cols = slice(t * P, (t + 1) * P)
+            b_ps = psum_b.tile([P, S], F32, name="b_ps")
+            nc.tensor.matmul_mx(out=b_ps[:], lhsT=winh_w[a][:, cols].bitcast(FP8X4), lhsT_scale=winh_sc[a][:, cols],
+                                rhs=v2_w[:].bitcast(FP8X4), rhs_scale=v2_sc[:], start=True, stop=True)
+            nc.scalar.activation(inh[a][:, t, :], b_ps[:], ACT.Square)
+
+        def substrate(a, t):
+            a_ps = psum_a.tile([P, S], F32, name="a_ps")
+            for g in range(2):
+                nc.tensor.matmul_mx(out=a_ps[:], lhsT=wsub_w[a][:, g, 2 * t * P : 2 * (t + 1) * P].bitcast(FP4X4),
+                                    lhsT_scale=wsub_s[a][:, g, t * P : (t + 1) * P],
+                                    rhs=v_w[g][:].bitcast(FP8X4), rhs_scale=v_sc[:, g * S : (g + 1) * S],
+                                    start=(g == 0), stop=(g == 1))
+            nc.scalar.activation(sub[a][:, t, :], a_ps[:], ACT.Square)
+
+        def quotient(a, t):
+            total = ring.tile([P, S], F32, name="total")
+            nc.vector.tensor_tensor(total[:], sub[a][:, t, :], inh[a][:, t, :], ALU.add)
+            nc.scalar.activation(root[a][:, t, :], total[:], ACT.Abs_reciprocal_sqrt, bias=one[:])
+            nc.vector.scalar_tensor_tensor(part[a][:, t, :], sub[a][:, t, :], rate[:, a, t : t + 1], root[a][:, t, :],
+                                           ALU.mult, ALU.mult)
+
+        def rates(a, u):
+            cols = slice(u * HALF, (u + 1) * HALF)
+            h_bf = ring.tile([P, HALF, PACK], BF16, name="h_bf", align_bytes=64)
+            nc.vector.tensor_tensor(h_bf[:].rearrange("p (c i) t -> p c t i", i=4),
+                                    part[a][:, :, cols].rearrange("p t (c i) -> p c t i", i=4),
+                                    root[a][:, :, cols].rearrange("p t (c i) -> p c t i", i=4), ALU.mult)
+            nc.vector.quantize_mx(out=h_w[a][u][:].bitcast(FP8X4), scales=h_sc[a][u][:],
+                                  in_=h_bf[:].rearrange("p j t -> p (j t)"))
+
+        def readout(u):
+            for pair in range(2):
+                o_ps = psum_o.tile([P, 2, HALF], F32, name="o_ps")
+                for e in range(2):
+                    cols = slice((2 * pair + e) * P, (2 * pair + e + 1) * P)
+                    for a in range(2):
+                        nc.tensor.matmul_mx(out=o_ps[:, e, :], lhsT=wread_w[:, a, cols].bitcast(FP8X4),
+                                            lhsT_scale=wread_sc[:, a, cols], rhs=h_w[a][u][:].bitcast(FP8X4),
+                                            rhs_scale=h_sc[a][u][:], start=(a == 0), stop=(a == 1))
+                result = held([P, 2, HALF], F32, "result%d%d" % (u, pair))
+                if u == 1 and pair == 1:
+                    nc.vector.tensor_copy(result[:], o_ps[:])
+                else:
+                    nc.scalar.copy(result[:], o_ps[:])
+                nc.sync.dma_start(
+                    out[2 * pair * P : 2 * (pair + 1) * P, u * HALF : (u + 1) * HALF].rearrange("(e p) j -> p e j", e=2),
+                    result[:])
+
+        prepare_winh(0)
+        for t in range(PACK):
+            inhibitor(0, t)
+        nc.vector.tensor_copy(v_w[0][:], tab_w[0][:].bitcast(U32).indirect(lists[:]))
+        prepare_wsub(0)
+        nc.vector.tensor_copy(v_w[1][:], tab_w[1][:].bitcast(U32).indirect(lists[:]))
+        late = shared([P, PACK, PASS], F32, "winh_late", "table0")
+        nc.sync.dma_start(late[:], winh_rows[:, :, PASS:])
+        winh_raw.append([late[:, :, u * PASS // 2 : (u + 1) * PASS // 2] for u in range(2)])
+        load_wsub(1)
+        wread_w = shared([P, 2, N], I32, "wread_w", "table1")
+        nc.sync.dma_start(wread_w[:], wread_words.rearrange("g p c i -> p g (c i)").bitcast(I32))
+        load_scale_rows(nc.sync, wread_sc[:].bitcast(I32), wread_scales.bitcast(I32), 0)
+        for t in range(PACK):
+            substrate(0, t)
+            quotient(0, t)
+        prepare_winh(1)
+        prepare_wsub(1)
+        for u in range(2):
+            rates(0, u)
+        for t in range(PACK):
+            substrate(1, t)
+            inhibitor(1, t)
+            quotient(1, t)
+        for u in range(2):
+            rates(1, u)
+            readout(u)

@@ -32,20 +32,19 @@ def tile_list_competitive_inhibitor_assay_kernel(
     with ExitStack() as ctx:
         keep = ctx.enter_context(tc.tile_pool(name="keep", bufs=1))
         ring = ctx.enter_context(tc.tile_pool(name="ring", bufs=3))
-        psum_a = ctx.enter_context(tc.psum_pool(name="psum_a", bufs=3))
-        psum_b = ctx.enter_context(tc.psum_pool(name="psum_b", bufs=3))
-        psum_o = ctx.enter_context(tc.psum_pool(name="psum_o", bufs=2))
+        psum = ctx.enter_context(tc.psum_pool(name="psum", bufs=1))
+
+        def bank(i, shape):
+            return psum.tile(shape, F32, name="bank%d" % i)
 
         def held(shape, dtype, name):
             return keep.tile(shape, dtype, name=name, align_bytes=64)
 
         lists = keep.tile([P, S // 16], U16, name="lists")
         list2 = keep.tile([P, S // 16], U16, name="list2")
-        nc.sync.dma_start(lists[:], offs)
-        nc.sync.dma_start(list2[:], offs2)
 
         one = held([P, 1], F32, "one")
-        warm = keep.tile([P, 1], F32, name="warm", tag="table0", align_bytes=64)
+        warm = held([P, 1], F32, "warm")
 
         tab_sc = held([P, 2 * T], U8, "tab_sc")
         tab2_sc = held([P, T2], U8, "tab2_sc")
@@ -60,8 +59,8 @@ def tile_list_competitive_inhibitor_assay_kernel(
         nc.vector.memset(v_sc[:].bitcast(I32), 0)
         nc.vector.memset(wread_sc[:].bitcast(I32), 0)
 
-        def load_scale_rows(queue, dst, src, first):
-            for d in range(QUADS):
+        def load_scale_rows(queue, dst, src, first, quads=range(QUADS)):
+            for d in quads:
                 queue.dma_start(dst[32 * d + first : 32 * d + first + 4],
                                 src[:, 4 * d : 4 * d + 4, :].rearrange("a q c -> q a c"))
 
@@ -71,30 +70,36 @@ def tile_list_competitive_inhibitor_assay_kernel(
 
         winh_rows = winh.rearrange("(p j) c -> p j c", j=PACK)
         rate = held([P, 2, PACK], F32, "rate")
-        winh_raw, wsub_raw = [], []
+        winh_cuts = [[0, PASS // 2, PASS], [PASS, 2 * PASS]]
+        winh_raw = {}
+        wsub_raw = [held([P, 2, 2 * PASS], U8, "wsub_raw%d" % a) for a in range(2)]
+        tab2_w = held([P, T2], I32, "tab2_w")
+        tab_w = [held([P, T], I32, "tab_w%d" % g) for g in range(2)]
+        wread_w = held([P, 2, N], I32, "wread_w")
 
-        def shared(shape, dtype, name, tag):
-            return keep.tile(shape, dtype, name=name, tag=tag, align_bytes=64)
+        def load_winh(a, u):
+            c0, c1 = winh_cuts[a][u : u + 2]
+            winh_raw[a, u] = held([P, PACK, c1 - c0], F32, "winh_raw%d%d" % (a, u))
+            nc.sync.dma_start(winh_raw[a, u][:], winh_rows[:, :, c0:c1])
 
         def load_wsub(a):
-            raw = shared([P, 2, 2 * PASS], U8, "wsub_raw%d" % a, "wsub_raw")
-            nc.sync.dma_start(raw[:].bitcast(I32),
+            nc.sync.dma_start(wsub_raw[a][:].bitcast(I32),
                               wsub_words.bitcast(I32)[:, :, a * PASS // 2 : (a + 1) * PASS // 2].rearrange("g p c -> p g c"))
-            wsub_raw.append(raw)
 
-        nc.sync.dma_start(rate[:], vmax.rearrange("(a p t) -> p a t", a=2, t=PACK))
-        load_wsub(0)
-        tab2_w = shared([P, T2], I32, "tab2_w", "table1")
+        nc.sync.dma_start(list2[:], offs2)
+        nc.sync.dma_start(lists[:], offs)
         nc.sync.dma_start(tab2_w[:], words(tab2_words[0]))
-        winh_raw.append([held([P, PACK, PASS // 2], F32, "winh_raw%d" % u)[:] for u in range(2)])
-        for u in range(2):
-            nc.sync.dma_start(winh_raw[0][u], winh_rows[:, :, u * PASS // 2 : (u + 1) * PASS // 2])
+        load_winh(0, 0)
         load_scale_rows(nc.sync, tab_sc[:].bitcast(I32).rearrange("p (a c) -> p a c", a=2),
                         tab_scales.bitcast(I32), SHIFT)
-        tab_w = [shared([P, T], I32, "tab_w0", "table0")]
+        load_winh(0, 1)
+        tab2_rows = tab2_sc[:].bitcast(I32).rearrange("p (a c) -> p a c", a=1)
+        load_scale_rows(nc.sync, tab2_rows, tab2_scales.bitcast(I32), 0, range(1))
+        load_winh(1, 0)
+        load_scale_rows(nc.sync, tab2_rows, tab2_scales.bitcast(I32), 0, range(1, QUADS))
         nc.sync.dma_start(tab_w[0][:], words(tab_words[0]))
-        load_scale_rows(nc.sync, tab2_sc[:].bitcast(I32).rearrange("p (a c) -> p a c", a=1),
-                        tab2_scales.bitcast(I32), 0)
+        load_wsub(0)
+        load_scale_rows(nc.sync, wsub_sc[:].bitcast(I32), wsub_scales.bitcast(I32), 0)
 
         v2_w = held([P, S], U32, "v2_w")
         v2_sc = held([P, S], U8, "v2_sc")
@@ -102,24 +107,27 @@ def tile_list_competitive_inhibitor_assay_kernel(
         tab_sc1 = held([P, T], U8, "tab_sc1")
         picked_sc = held([P, 2 * S], U8, "picked_sc")
         nc.vector.tensor_copy(v2_w[:], tab2_w[:].bitcast(U32).indirect(list2[:]))
-        tab_w.append(shared([P, T], I32, "tab_w1", "table1"))
-        nc.sync.dma_start(tab_w[1][:], words(tab_words[1]))
-        load_scale_rows(nc.sync, wsub_sc[:].bitcast(I32), wsub_scales.bitcast(I32), 0)
         nc.vector.tensor_copy(tab_sc1[:].bitcast(I32), tab_sc[:].bitcast(I32)[:, T // 4 :])
         nc.vector.tensor_copy(picked_sc[:, :S], tab_sc[:].indirect(lists[:]))
         nc.vector.tensor_copy(picked_sc[:, S:], tab_sc1[:].indirect(lists[:]))
         rows = 112
         nc.sync.dma_start(v_sc[:rows].bitcast(I32), picked_sc[SHIFT : SHIFT + rows].bitcast(I32))
+        nc.sync.dma_start(tab_w[1][:], words(tab_words[1]))
+        nc.sync.dma_start(rate[:], vmax.rearrange("(a p t) -> p a t", a=2, t=PACK))
+        load_wsub(1)
+        nc.sync.dma_start(wread_w[:], wread_words.rearrange("g p c i -> p g (c i)").bitcast(I32))
+        load_scale_rows(nc.sync, wread_sc[:].bitcast(I32), wread_scales.bitcast(I32), 0)
+
         nc.vector.tensor_copy(v2_sc[:], tab2_sc[:].indirect(list2[:]))
 
         winh_w, winh_sc, wsub_w, wsub_s = [], [], [], []
 
         def prepare_winh(a):
             grouped = held([P, PACK, P, PACK], BF16, "winh_bf%d" % a)
-            for u in range(2):
-                nc.scalar.activation(
-                    grouped[:, :, u * P // 2 : (u + 1) * P // 2, :].rearrange("p t m j -> p m j t"),
-                    winh_raw[a][u].rearrange("p j (m t) -> p m j t", t=PACK), ACT.Copy)
+            for u in range(len(winh_cuts[a]) - 1):
+                m0, m1 = [(c - a * PASS) // PACK for c in winh_cuts[a][u : u + 2]]
+                nc.scalar.activation(grouped[:, :, m0:m1, :].rearrange("p t m j -> p m j t"),
+                                     winh_raw[a, u][:].rearrange("p j (m t) -> p m j t", t=PACK), ACT.Copy)
             codes = held([P, PASS], U32, "winh_w%d" % a)
             scales = held([P, PASS], U8, "winh_sc%d" % a)
             nc.vector.quantize_mx(out=codes[:].bitcast(FP8X4), scales=scales[:],
@@ -139,85 +147,97 @@ def tile_list_competitive_inhibitor_assay_kernel(
 
         inh = [held([P, PACK, S], F32, "inh%d" % a) for a in range(2)]
         sub = [held([P, PACK, S], F32, "sub%d" % a) for a in range(2)]
-        root = [held([P, PACK, S], F32, "root%d" % a) for a in range(2)]
-        part = [held([P, PACK, S], F32, "part%d" % a) for a in range(2)]
-        h_w = [[held([P, HALF], U32, "h_w%d%d" % (a, u)) for u in range(2)] for a in range(2)]
-        h_sc = [[held([P, HALF], U8, "h_sc%d%d" % (a, u)) for u in range(2)] for a in range(2)]
+        right = [held([P, PACK, S], F32, "right%d" % a) for a in range(2)]
+        left = [held([P, PACK, S], F32, "left%d" % a) for a in range(2)]
+        h_w, h_sc = {}, {}
 
         def inhibitor(a, t):
             cols = slice(t * P, (t + 1) * P)
-            b_ps = psum_b.tile([P, S], F32, name="b_ps")
+            b_ps = bank(t, [P, S])
             nc.tensor.matmul_mx(out=b_ps[:], lhsT=winh_w[a][:, cols].bitcast(FP8X4), lhsT_scale=winh_sc[a][:, cols],
                                 rhs=v2_w[:].bitcast(FP8X4), rhs_scale=v2_sc[:], start=True, stop=True)
             nc.scalar.activation(inh[a][:, t, :], b_ps[:], ACT.Square)
 
-        def substrate(a, t):
-            a_ps = psum_a.tile([P, S], F32, name="a_ps")
-            for g in range(2):
-                nc.tensor.matmul_mx(out=a_ps[:], lhsT=wsub_w[a][:, g, 2 * t * P : 2 * (t + 1) * P].bitcast(FP4X4),
-                                    lhsT_scale=wsub_s[a][:, g, t * P : (t + 1) * P],
-                                    rhs=v_w[g][:].bitcast(FP8X4), rhs_scale=v_sc[:, g * S : (g + 1) * S],
-                                    start=(g == 0), stop=(g == 1))
-            nc.scalar.activation(sub[a][:, t, :], a_ps[:], ACT.Square)
+        def substrate_pass(a_ps, a, t, g):
+            nc.tensor.matmul_mx(out=a_ps[:], lhsT=wsub_w[a][:, g, 2 * t * P : 2 * (t + 1) * P].bitcast(FP4X4),
+                                lhsT_scale=wsub_s[a][:, g, t * P : (t + 1) * P],
+                                rhs=v_w[g][:].bitcast(FP8X4), rhs_scale=v_sc[:, g * S : (g + 1) * S],
+                                start=(g == 0), stop=(g == 1))
 
-        def quotient(a, t):
+        def quotient(a, t, a_ps, on_scalar):
             total = ring.tile([P, S], F32, name="total")
+            nc.scalar.activation(sub[a][:, t, :], a_ps[:], ACT.Square)
             nc.vector.tensor_tensor(total[:], sub[a][:, t, :], inh[a][:, t, :], ALU.add)
-            nc.scalar.activation(root[a][:, t, :], total[:], ACT.Abs_reciprocal_sqrt, bias=one[:])
-            nc.vector.scalar_tensor_tensor(part[a][:, t, :], sub[a][:, t, :], rate[:, a, t : t + 1], root[a][:, t, :],
-                                           ALU.mult, ALU.mult)
+            if on_scalar:
+                root = ring.tile([P, S], F32, name="root")
+                nc.scalar.activation(left[a][:, t, :], sub[a][:, t, :], ACT.Copy, scale=rate[:, a, t : t + 1])
+                nc.scalar.activation(root[:], total[:], ACT.Abs_reciprocal_sqrt, bias=one[:])
+                nc.scalar.activation(right[a][:, t, :], root[:], ACT.Square)
+            else:
+                nc.scalar.activation(right[a][:, t, :], total[:], ACT.Abs_reciprocal_sqrt, bias=one[:])
+                nc.vector.scalar_tensor_tensor(left[a][:, t, :], sub[a][:, t, :], rate[:, a, t : t + 1],
+                                               right[a][:, t, :], ALU.mult, ALU.mult)
 
-        def rates(a, u):
-            cols = slice(u * HALF, (u + 1) * HALF)
-            h_bf = ring.tile([P, HALF, PACK], BF16, name="h_bf", align_bytes=64)
+        def rates(a, j0, width):
+            cols = slice(j0, j0 + width)
+            h_bf = ring.tile([P, width, PACK], BF16, name="h_bf", align_bytes=64)
             nc.vector.tensor_tensor(h_bf[:].rearrange("p (c i) t -> p c t i", i=4),
-                                    part[a][:, :, cols].rearrange("p t (c i) -> p c t i", i=4),
-                                    root[a][:, :, cols].rearrange("p t (c i) -> p c t i", i=4), ALU.mult)
-            nc.vector.quantize_mx(out=h_w[a][u][:].bitcast(FP8X4), scales=h_sc[a][u][:],
+                                    left[a][:, :, cols].rearrange("p t (c i) -> p c t i", i=4),
+                                    right[a][:, :, cols].rearrange("p t (c i) -> p c t i", i=4), ALU.mult)
+            h_w[a, j0] = held([P, width], U32, "h_w%d_%d" % (a, j0))
+            h_sc[a, j0] = held([P, width], U8, "h_sc%d_%d" % (a, j0))
+            nc.vector.quantize_mx(out=h_w[a, j0][:].bitcast(FP8X4), scales=h_sc[a, j0][:],
                                   in_=h_bf[:].rearrange("p j t -> p (j t)"))
 
-        def readout(u):
-            for pair in range(2):
-                o_ps = psum_o.tile([P, 2, HALF], F32, name="o_ps")
-                for e in range(2):
-                    cols = slice((2 * pair + e) * P, (2 * pair + e + 1) * P)
-                    for a in range(2):
-                        nc.tensor.matmul_mx(out=o_ps[:, e, :], lhsT=wread_w[:, a, cols].bitcast(FP8X4),
-                                            lhsT_scale=wread_sc[:, a, cols], rhs=h_w[a][u][:].bitcast(FP8X4),
-                                            rhs_scale=h_sc[a][u][:], start=(a == 0), stop=(a == 1))
-                result = held([P, 2, HALF], F32, "result%d%d" % (u, pair))
-                if u == 1 and pair == 1:
-                    nc.vector.tensor_copy(result[:], o_ps[:])
-                else:
-                    nc.scalar.copy(result[:], o_ps[:])
-                nc.sync.dma_start(
-                    out[2 * pair * P : 2 * (pair + 1) * P, u * HALF : (u + 1) * HALF].rearrange("(e p) j -> p e j", e=2),
-                    result[:])
+        def readout_pass(o_ps, n, a, j0, start, stop):
+            cols = slice(n * P, (n + 1) * P)
+            nc.tensor.matmul_mx(out=o_ps, lhsT=wread_w[:, a, cols].bitcast(FP8X4),
+                                lhsT_scale=wread_sc[:, a, cols], rhs=h_w[a, j0][:].bitcast(FP8X4),
+                                rhs_scale=h_sc[a, j0][:], start=start, stop=stop)
 
-        prepare_winh(0)
-        for t in range(PACK):
-            inhibitor(0, t)
+        for a in range(2):
+            prepare_winh(a)
+        for a in range(2):
+            for t in range(PACK):
+                inhibitor(a, t)
         nc.vector.tensor_copy(v_w[0][:], tab_w[0][:].bitcast(U32).indirect(lists[:]))
         prepare_wsub(0)
+        a_ps = [bank(PACK + t, [P, S]) for t in range(PACK)]
+        for t in range(PACK):
+            substrate_pass(a_ps[t], 0, t, 0)
         nc.vector.tensor_copy(v_w[1][:], tab_w[1][:].bitcast(U32).indirect(lists[:]))
-        late = shared([P, PACK, PASS], F32, "winh_late", "table0")
-        nc.sync.dma_start(late[:], winh_rows[:, :, PASS:])
-        winh_raw.append([late[:, :, u * PASS // 2 : (u + 1) * PASS // 2] for u in range(2)])
-        load_wsub(1)
-        wread_w = shared([P, 2, N], I32, "wread_w", "table1")
-        nc.sync.dma_start(wread_w[:], wread_words.rearrange("g p c i -> p g (c i)").bitcast(I32))
-        load_scale_rows(nc.sync, wread_sc[:].bitcast(I32), wread_scales.bitcast(I32), 0)
-        for t in range(PACK):
-            substrate(0, t)
-            quotient(0, t)
-        prepare_winh(1)
         prepare_wsub(1)
-        for u in range(2):
-            rates(0, u)
         for t in range(PACK):
-            substrate(1, t)
-            inhibitor(1, t)
-            quotient(1, t)
-        for u in range(2):
-            rates(1, u)
-            readout(u)
+            substrate_pass(a_ps[t], 0, t, 1)
+            quotient(0, t, a_ps[t], False)
+        for j0 in (0, HALF):
+            rates(0, j0, HALF)
+        for t in range(PACK):
+            a_ps = bank(PACK + t, [P, S])
+            for g in range(2):
+                substrate_pass(a_ps, 1, t, g)
+            quotient(1, t, a_ps, t >= 2)
+        early = [bank(PACK + n, [P, HALF]) for n in range(4)]
+        late = [bank(n, [P, HALF]) for n in range(4)]
+        for n in range(4):
+            readout_pass(late[n][:], n, 0, HALF, True, False)
+        for n in range(4):
+            readout_pass(early[n][:], n, 0, 0, True, False)
+        rates(1, 0, HALF)
+        first = held([P, 4, HALF], F32, "first")
+        for n in range(4):
+            readout_pass(early[n][:], n, 1, 0, False, True)
+            nc.scalar.copy(first[:, n, :], early[n][:])
+        nc.sync.dma_start(out[:, :HALF].rearrange("(n p) j -> p n j", p=P), first[:])
+        rates(1, HALF, P)
+        for n in range(4):
+            readout_pass(late[n][:, :P], n, 1, HALF, False, False)
+        rates(1, HALF + P, P)
+        for n in range(4):
+            readout_pass(late[n][:, P:], n, 1, HALF + P, False, True)
+            result = held([P, HALF], F32, "last%d" % n)
+            if n % 2:
+                nc.vector.tensor_copy(result[:], late[n][:])
+            else:
+                nc.scalar.copy(result[:], late[n][:])
+            nc.sync.dma_start(out[n * P : (n + 1) * P, HALF:], result[:])

@@ -70,11 +70,12 @@ def tile_list_competitive_inhibitor_assay_kernel(
 
         winh_rows = winh.rearrange("(p j) c -> p j c", j=PACK)
         rate = held([P, 2, PACK], F32, "rate")
-        winh_cuts = [[0, PASS // 2, PASS], [PASS, 2 * PASS]]
+        winh_cuts = [[0, PASS // 2, PASS], [PASS, 3 * PASS // 2, 2 * PASS]]
         winh_raw = {}
         wsub_raw = [held([P, 2, 2 * PASS], U8, "wsub_raw%d" % a) for a in range(2)]
         tab2_w = held([P, T2], I32, "tab2_w")
         tab_w = [held([P, T], I32, "tab_w%d" % g) for g in range(2)]
+        scale_homes = ["wsub_s0", "tab_w1"]
         wread_w = held([P, 2, N], I32, "wread_w")
 
         def load_winh(a, u):
@@ -97,6 +98,7 @@ def tile_list_competitive_inhibitor_assay_kernel(
         load_scale_rows(nc.sync, tab2_rows, tab2_scales.bitcast(I32), 0, range(1))
         load_winh(1, 0)
         load_scale_rows(nc.sync, tab2_rows, tab2_scales.bitcast(I32), 0, range(1, QUADS))
+        load_winh(1, 1)
         nc.sync.dma_start(tab_w[0][:], words(tab_words[0]))
         load_wsub(0)
         load_scale_rows(nc.sync, wsub_sc[:].bitcast(I32), wsub_scales.bitcast(I32), 0)
@@ -126,8 +128,9 @@ def tile_list_competitive_inhibitor_assay_kernel(
             grouped = held([P, PACK, P, PACK], BF16, "winh_bf%d" % a)
             for u in range(len(winh_cuts[a]) - 1):
                 m0, m1 = [(c - a * PASS) // PACK for c in winh_cuts[a][u : u + 2]]
-                nc.scalar.activation(grouped[:, :, m0:m1, :].rearrange("p t m j -> p m j t"),
-                                     winh_raw[a, u][:].rearrange("p j (m t) -> p m j t", t=PACK), ACT.Copy)
+                cast = nc.vector.tensor_copy if (a, u) == (1, 1) else nc.scalar.copy
+                cast(grouped[:, :, m0:m1, :].rearrange("p t m j -> p m j t"),
+                     winh_raw[a, u][:].rearrange("p j (m t) -> p m j t", t=PACK))
             codes = held([P, PASS], U32, "winh_w%d" % a)
             scales = held([P, PASS], U8, "winh_sc%d" % a)
             nc.vector.quantize_mx(out=codes[:].bitcast(FP8X4), scales=scales[:],
@@ -137,7 +140,7 @@ def tile_list_competitive_inhibitor_assay_kernel(
 
         def prepare_wsub(a):
             codes = held([P, 2, 2 * PASS], U8, "wsub_w%d" % a)
-            scales = held([P, 2, PASS], U8, "wsub_s%d" % a)
+            scales = keep.tile([P, 2, PASS], U8, name="wsub_s%d" % a, tag=scale_homes[a], align_bytes=64)
             nc.vector.tensor_copy(codes[:].bitcast(U16).rearrange("p g (t m) -> p g m t", t=PACK),
                                   wsub_raw[a][:].bitcast(U16).rearrange("p g (m t) -> p g m t", t=PACK))
             nc.vector.tensor_copy(scales[:].rearrange("p g (t m) -> p g m t", t=PACK),
@@ -153,7 +156,7 @@ def tile_list_competitive_inhibitor_assay_kernel(
 
         def inhibitor(a, t):
             cols = slice(t * P, (t + 1) * P)
-            b_ps = bank(t, [P, S])
+            b_ps = bank(PACK * a + t, [P, S])
             nc.tensor.matmul_mx(out=b_ps[:], lhsT=winh_w[a][:, cols].bitcast(FP8X4), lhsT_scale=winh_sc[a][:, cols],
                                 rhs=v2_w[:].bitcast(FP8X4), rhs_scale=v2_sc[:], start=True, stop=True)
             nc.scalar.activation(inh[a][:, t, :], b_ps[:], ACT.Square)
@@ -184,6 +187,9 @@ def tile_list_competitive_inhibitor_assay_kernel(
             nc.vector.tensor_tensor(h_bf[:].rearrange("p (c i) t -> p c t i", i=4),
                                     left[a][:, :, cols].rearrange("p t (c i) -> p c t i", i=4),
                                     right[a][:, :, cols].rearrange("p t (c i) -> p c t i", i=4), ALU.mult)
+            return h_bf
+
+        def quantize_rates(a, j0, width, h_bf):
             h_w[a, j0] = held([P, width], U32, "h_w%d_%d" % (a, j0))
             h_sc[a, j0] = held([P, width], U8, "h_sc%d_%d" % (a, j0))
             nc.vector.quantize_mx(out=h_w[a, j0][:].bitcast(FP8X4), scales=h_sc[a, j0][:],
@@ -202,7 +208,7 @@ def tile_list_competitive_inhibitor_assay_kernel(
                 inhibitor(a, t)
         nc.vector.tensor_copy(v_w[0][:], tab_w[0][:].bitcast(U32).indirect(lists[:]))
         prepare_wsub(0)
-        a_ps = [bank(PACK + t, [P, S]) for t in range(PACK)]
+        a_ps = [bank(t, [P, S]) for t in range(PACK)]
         for t in range(PACK):
             substrate_pass(a_ps[t], 0, t, 0)
         nc.vector.tensor_copy(v_w[1][:], tab_w[1][:].bitcast(U32).indirect(lists[:]))
@@ -210,8 +216,9 @@ def tile_list_competitive_inhibitor_assay_kernel(
         for t in range(PACK):
             substrate_pass(a_ps[t], 0, t, 1)
             quotient(0, t, a_ps[t], False)
-        for j0 in (0, HALF):
-            rates(0, j0, HALF)
+        halves = [rates(0, j0, HALF) for j0 in (0, HALF)]
+        for u in range(2):
+            quantize_rates(0, u * HALF, HALF, halves[u])
         for t in range(PACK):
             a_ps = bank(PACK + t, [P, S])
             for g in range(2):
@@ -223,16 +230,19 @@ def tile_list_competitive_inhibitor_assay_kernel(
             readout_pass(late[n][:], n, 0, HALF, True, False)
         for n in range(4):
             readout_pass(early[n][:], n, 0, 0, True, False)
-        rates(1, 0, HALF)
-        first = held([P, 4, HALF], F32, "first")
+        h_early = rates(1, 0, HALF)
+        h_next = rates(1, HALF, P)
+        quantize_rates(1, 0, HALF, h_early)
+        h_last = rates(1, HALF + P, P)
         for n in range(4):
             readout_pass(early[n][:], n, 1, 0, False, True)
-            nc.scalar.copy(first[:, n, :], early[n][:])
-        nc.sync.dma_start(out[:, :HALF].rearrange("(n p) j -> p n j", p=P), first[:])
-        rates(1, HALF, P)
+            result = held([P, HALF], F32, "first%d" % n)
+            nc.scalar.copy(result[:], early[n][:])
+            nc.sync.dma_start(out[n * P : (n + 1) * P, :HALF], result[:])
+        quantize_rates(1, HALF, P, h_next)
         for n in range(4):
             readout_pass(late[n][:, :P], n, 1, HALF, False, False)
-        rates(1, HALF + P, P)
+        quantize_rates(1, HALF + P, P, h_last)
         for n in range(4):
             readout_pass(late[n][:, P:], n, 1, HALF + P, False, True)
             result = held([P, HALF], F32, "last%d" % n)

@@ -20,8 +20,9 @@ P = 128
 PACK = 4
 PASS = P * PACK
 QUADS = 4
-SHIFT = 14
 HALF = S // 2
+TAB2_ROW = 4
+WREAD_ROW = 8
 
 
 def tile_list_competitive_inhibitor_assay_kernel(
@@ -31,105 +32,101 @@ def tile_list_competitive_inhibitor_assay_kernel(
     nc = tc.nc
     with ExitStack() as ctx:
         keep = ctx.enter_context(tc.tile_pool(name="keep", bufs=1))
-        ring = ctx.enter_context(tc.tile_pool(name="ring", bufs=3))
         psum = ctx.enter_context(tc.psum_pool(name="psum", bufs=1))
 
         def bank(i, shape):
             return psum.tile(shape, F32, name="bank%d" % i)
 
-        def held(shape, dtype, name):
-            return keep.tile(shape, dtype, name=name, align_bytes=64)
+        def held(shape, dtype, name, tag=None):
+            return keep.tile(shape, dtype, name=name, tag=tag or name, align_bytes=64)
 
         lists = keep.tile([P, S // 16], U16, name="lists")
         list2 = keep.tile([P, S // 16], U16, name="list2")
 
+        seed = held([P, 1], F32, "seed")
         one = held([P, 1], F32, "one")
-        warm = held([P, 1], F32, "warm")
 
-        tab_sc = held([P, 2 * T], U8, "tab_sc")
+        tab_sc = held([P, T], U8, "tab_sc")
         tab2_sc = held([P, T2], U8, "tab2_sc")
         wsub_sc = held([P, 2, H], U8, "wsub_sc")
         wread_sc = held([P, 2, N], U8, "wread_sc")
-        v_sc = held([P, 2 * S], U8, "v_sc")
+        v_sc = held([P, 2, S], U8, "v_sc")
         nc.vector.memset(tab_sc[:].bitcast(I32), 0)
-        nc.vector.memset(one[:], 1.0)
-        nc.scalar.activation(warm[:], one[:], ACT.Abs_reciprocal_sqrt, bias=one[:])
-        nc.vector.memset(wsub_sc[:].bitcast(I32), 0)
         nc.vector.memset(tab2_sc[:].bitcast(I32), 0)
+        nc.vector.memset(seed[:], 1.0)
         nc.vector.memset(v_sc[:].bitcast(I32), 0)
-        nc.vector.memset(wread_sc[:].bitcast(I32), 0)
+        nc.gpsimd.memset(wsub_sc[:].bitcast(I32), 0)
+        nc.gpsimd.memset(wread_sc[:].bitcast(I32), 0)
 
-        def load_scale_rows(queue, dst, src, first, quads=range(QUADS)):
-            for d in quads:
+        def load_scale_rows(queue, dst, src, first):
+            for d in range(QUADS):
                 queue.dma_start(dst[32 * d + first : 32 * d + first + 4],
                                 src[:, 4 * d : 4 * d + 4, :].rearrange("a q c -> q a c"))
-
 
         def words(src):
             return src.rearrange("p t i -> p (t i)").bitcast(I32)
 
         winh_rows = winh.rearrange("(p j) c -> p j c", j=PACK)
         rate = held([P, 2, PACK], F32, "rate")
-        winh_cuts = [[0, PASS // 2, PASS], [PASS, 3 * PASS // 2, 2 * PASS]]
         winh_raw = {}
         wsub_raw = [held([P, 2, 2 * PASS], U8, "wsub_raw%d" % a) for a in range(2)]
         tab2_w = held([P, T2], I32, "tab2_w")
         tab_w = [held([P, T], I32, "tab_w%d" % g) for g in range(2)]
-        scale_homes = ["wsub_s0", "tab_w1"]
         wread_w = held([P, 2, N], I32, "wread_w")
 
         def load_winh(a, u):
-            c0, c1 = winh_cuts[a][u : u + 2]
-            winh_raw[a, u] = held([P, PACK, c1 - c0], F32, "winh_raw%d%d" % (a, u))
-            nc.sync.dma_start(winh_raw[a, u][:], winh_rows[:, :, c0:c1])
+            c0 = a * PASS + u * PASS // 2
+            winh_raw[a, u] = held([P, PACK, PASS // 2], F32, "winh_raw%d%d" % (a, u))
+            nc.sync.dma_start(winh_raw[a, u][:], winh_rows[:, :, c0 : c0 + PASS // 2])
 
         def load_wsub(a):
             nc.sync.dma_start(wsub_raw[a][:].bitcast(I32),
                               wsub_words.bitcast(I32)[:, :, a * PASS // 2 : (a + 1) * PASS // 2].rearrange("g p c -> p g c"))
 
-        nc.sync.dma_start(list2[:], offs2)
+        picked_sc = held([P, S], U8, "picked_sc")
+
+        def move_scales(g):
+            for i in range(4):
+                nc.sync.dma_start(v_sc[i:P:32, g, :].bitcast(I32), picked_sc[8 * i + 4 * g : P : 32].bitcast(I32))
+
         nc.sync.dma_start(lists[:], offs)
+        nc.sync.dma_start(list2[:], offs2)
+        for g in range(2):
+            nc.scalar.dma_start(tab_sc[4 * g : P : 8].bitcast(I32), tab_scales[g].bitcast(I32))
+        load_scale_rows(nc.scalar, tab2_sc[:].bitcast(I32).rearrange("p (a c) -> p a c", a=1),
+                        tab2_scales.bitcast(I32), TAB2_ROW)
+        nc.scalar.activation(one[:], seed[:], ACT.Abs_reciprocal_sqrt)
+        load_scale_rows(nc.gpsimd, wsub_sc[:].bitcast(I32), wsub_scales.bitcast(I32), 0)
+        nc.gpsimd.dma_start(rate[:], vmax.rearrange("(a p t) -> p a t", a=2, t=PACK))
+        load_scale_rows(nc.gpsimd, wread_sc[:].bitcast(I32), wread_scales.bitcast(I32), WREAD_ROW)
         nc.sync.dma_start(tab2_w[:], words(tab2_words[0]))
         load_winh(0, 0)
-        load_scale_rows(nc.sync, tab_sc[:].bitcast(I32).rearrange("p (a c) -> p a c", a=2),
-                        tab_scales.bitcast(I32), SHIFT)
         load_winh(0, 1)
-        tab2_rows = tab2_sc[:].bitcast(I32).rearrange("p (a c) -> p a c", a=1)
-        load_scale_rows(nc.sync, tab2_rows, tab2_scales.bitcast(I32), 0, range(1))
-        load_winh(1, 0)
-        load_scale_rows(nc.sync, tab2_rows, tab2_scales.bitcast(I32), 0, range(1, QUADS))
-        load_winh(1, 1)
         nc.sync.dma_start(tab_w[0][:], words(tab_words[0]))
-        load_wsub(0)
-        load_scale_rows(nc.sync, wsub_sc[:].bitcast(I32), wsub_scales.bitcast(I32), 0)
 
         v2_w = held([P, S], U32, "v2_w")
         v2_sc = held([P, S], U8, "v2_sc")
         v_w = [held([P, S], U32, "v_w%d" % g) for g in range(2)]
-        tab_sc1 = held([P, T], U8, "tab_sc1")
-        picked_sc = held([P, 2 * S], U8, "picked_sc")
-        nc.vector.tensor_copy(v2_w[:], tab2_w[:].bitcast(U32).indirect(list2[:]))
-        nc.vector.tensor_copy(tab_sc1[:].bitcast(I32), tab_sc[:].bitcast(I32)[:, T // 4 :])
-        nc.vector.tensor_copy(picked_sc[:, :S], tab_sc[:].indirect(lists[:]))
-        nc.vector.tensor_copy(picked_sc[:, S:], tab_sc1[:].indirect(lists[:]))
-        rows = 112
-        nc.sync.dma_start(v_sc[:rows].bitcast(I32), picked_sc[SHIFT : SHIFT + rows].bitcast(I32))
+        nc.vector.tensor_copy(picked_sc[:], tab_sc[:].indirect(lists[:]))
+        move_scales(0)
+        load_wsub(0)
         nc.sync.dma_start(tab_w[1][:], words(tab_words[1]))
-        nc.sync.dma_start(rate[:], vmax.rearrange("(a p t) -> p a t", a=2, t=PACK))
+        move_scales(1)
         load_wsub(1)
+        load_winh(1, 0)
+        load_winh(1, 1)
         nc.sync.dma_start(wread_w[:], wread_words.rearrange("g p c i -> p g (c i)").bitcast(I32))
-        load_scale_rows(nc.sync, wread_sc[:].bitcast(I32), wread_scales.bitcast(I32), 0)
 
+        nc.vector.tensor_copy(v2_w[:], tab2_w[:].bitcast(U32).indirect(list2[:]))
         nc.vector.tensor_copy(v2_sc[:], tab2_sc[:].indirect(list2[:]))
 
         winh_w, winh_sc, wsub_w, wsub_s = [], [], [], []
 
         def prepare_winh(a):
             grouped = held([P, PACK, P, PACK], BF16, "winh_bf%d" % a)
-            for u in range(len(winh_cuts[a]) - 1):
-                m0, m1 = [(c - a * PASS) // PACK for c in winh_cuts[a][u : u + 2]]
+            for u in range(2):
                 cast = nc.vector.tensor_copy if (a, u) == (1, 1) else nc.scalar.copy
-                cast(grouped[:, :, m0:m1, :].rearrange("p t m j -> p m j t"),
+                cast(grouped[:, :, u * P // 2 : (u + 1) * P // 2, :].rearrange("p t m j -> p m j t"),
                      winh_raw[a, u][:].rearrange("p j (m t) -> p m j t", t=PACK))
             codes = held([P, PASS], U32, "winh_w%d" % a)
             scales = held([P, PASS], U8, "winh_sc%d" % a)
@@ -138,52 +135,54 @@ def tile_list_competitive_inhibitor_assay_kernel(
             winh_w.append(codes)
             winh_sc.append(scales)
 
-        def prepare_wsub(a):
-            codes = held([P, 2, 2 * PASS], U8, "wsub_w%d" % a)
-            scales = keep.tile([P, 2, PASS], U8, name="wsub_s%d" % a, tag=scale_homes[a], align_bytes=64)
-            nc.vector.tensor_copy(codes[:].bitcast(U16).rearrange("p g (t m) -> p g m t", t=PACK),
-                                  wsub_raw[a][:].bitcast(U16).rearrange("p g (m t) -> p g m t", t=PACK))
+        def order_wsub_scales(a, home):
+            scales = held([P, 2, PASS], U8, "wsub_s%d" % a, home)
             nc.vector.tensor_copy(scales[:].rearrange("p g (t m) -> p g m t", t=PACK),
                                   wsub_sc[:, :, a * PASS : (a + 1) * PASS].rearrange("p g (m t) -> p g m t", t=PACK))
-            wsub_w.append(codes)
             wsub_s.append(scales)
+
+        def order_wsub_words(a):
+            codes = held([P, 2, 2 * PASS], U8, "wsub_w%d" % a)
+            nc.vector.tensor_copy(codes[:].bitcast(U16).rearrange("p g (t m) -> p g m t", t=PACK),
+                                  wsub_raw[a][:].bitcast(U16).rearrange("p g (m t) -> p g m t", t=PACK))
+            wsub_w.append(codes)
 
         inh = [held([P, PACK, S], F32, "inh%d" % a) for a in range(2)]
         sub = [held([P, PACK, S], F32, "sub%d" % a) for a in range(2)]
+        total = [held([P, PACK, S], F32, "total%d" % a) for a in range(2)]
         right = [held([P, PACK, S], F32, "right%d" % a) for a in range(2)]
         left = [held([P, PACK, S], F32, "left%d" % a) for a in range(2)]
+        root = held([P, PACK, HALF], F32, "root")
         h_w, h_sc = {}, {}
 
-        def inhibitor(a, t):
+        def inhibitor(a, t, b_ps):
             cols = slice(t * P, (t + 1) * P)
-            b_ps = bank(PACK * a + t, [P, S])
             nc.tensor.matmul_mx(out=b_ps[:], lhsT=winh_w[a][:, cols].bitcast(FP8X4), lhsT_scale=winh_sc[a][:, cols],
-                                rhs=v2_w[:].bitcast(FP8X4), rhs_scale=v2_sc[:], start=True, stop=True)
+                                rhs=v2_w[:].bitcast(FP8X4), rhs_scale=v2_sc[TAB2_ROW:P], start=True, stop=True)
             nc.scalar.activation(inh[a][:, t, :], b_ps[:], ACT.Square)
 
         def substrate_pass(a_ps, a, t, g):
             nc.tensor.matmul_mx(out=a_ps[:], lhsT=wsub_w[a][:, g, 2 * t * P : 2 * (t + 1) * P].bitcast(FP4X4),
                                 lhsT_scale=wsub_s[a][:, g, t * P : (t + 1) * P],
-                                rhs=v_w[g][:].bitcast(FP8X4), rhs_scale=v_sc[:, g * S : (g + 1) * S],
+                                rhs=v_w[g][:].bitcast(FP8X4), rhs_scale=v_sc[:, g, :],
                                 start=(g == 0), stop=(g == 1))
 
-        def quotient(a, t, a_ps, on_scalar):
-            total = ring.tile([P, S], F32, name="total")
-            nc.scalar.activation(sub[a][:, t, :], a_ps[:], ACT.Square)
-            nc.vector.tensor_tensor(total[:], sub[a][:, t, :], inh[a][:, t, :], ALU.add)
-            if on_scalar:
-                root = ring.tile([P, S], F32, name="root")
-                nc.scalar.activation(left[a][:, t, :], sub[a][:, t, :], ACT.Copy, scale=rate[:, a, t : t + 1])
-                nc.scalar.activation(root[:], total[:], ACT.Abs_reciprocal_sqrt, bias=one[:])
-                nc.scalar.activation(right[a][:, t, :], root[:], ACT.Square)
-            else:
-                nc.scalar.activation(right[a][:, t, :], total[:], ACT.Abs_reciprocal_sqrt, bias=one[:])
-                nc.vector.scalar_tensor_tensor(left[a][:, t, :], sub[a][:, t, :], rate[:, a, t : t + 1],
-                                               right[a][:, t, :], ALU.mult, ALU.mult)
+        def add_squares(a, t):
+            nc.vector.tensor_tensor(total[a][:, t, :], sub[a][:, t, :], inh[a][:, t, :], ALU.add)
+
+        def factors_on_both(a, t, cols):
+            nc.scalar.activation(right[a][:, t, cols], total[a][:, t, cols], ACT.Abs_reciprocal_sqrt, bias=one[:])
+            nc.vector.scalar_tensor_tensor(left[a][:, t, cols], sub[a][:, t, cols], rate[:, a, t : t + 1],
+                                           right[a][:, t, cols], ALU.mult, ALU.mult)
+
+        def factors_on_scalar(a, t, cols):
+            nc.scalar.activation(root[:, t, :], total[a][:, t, cols], ACT.Abs_reciprocal_sqrt, bias=one[:])
+            nc.scalar.activation(right[a][:, t, cols], root[:, t, :], ACT.Square)
+            nc.scalar.activation(left[a][:, t, cols], sub[a][:, t, cols], ACT.Copy, scale=rate[:, a, t : t + 1])
 
         def rates(a, j0, width):
             cols = slice(j0, j0 + width)
-            h_bf = ring.tile([P, width, PACK], BF16, name="h_bf", align_bytes=64)
+            h_bf = held([P, width, PACK], BF16, "h_bf%d_%d" % (a, j0))
             nc.vector.tensor_tensor(h_bf[:].rearrange("p (c i) t -> p c t i", i=4),
                                     left[a][:, :, cols].rearrange("p t (c i) -> p c t i", i=4),
                                     right[a][:, :, cols].rearrange("p t (c i) -> p c t i", i=4), ALU.mult)
@@ -195,59 +194,71 @@ def tile_list_competitive_inhibitor_assay_kernel(
             nc.vector.quantize_mx(out=h_w[a, j0][:].bitcast(FP8X4), scales=h_sc[a, j0][:],
                                   in_=h_bf[:].rearrange("p j t -> p (j t)"))
 
-        def readout_pass(o_ps, n, a, j0, start, stop):
-            cols = slice(n * P, (n + 1) * P)
-            nc.tensor.matmul_mx(out=o_ps, lhsT=wread_w[:, a, cols].bitcast(FP8X4),
-                                lhsT_scale=wread_sc[:, a, cols], rhs=h_w[a, j0][:].bitcast(FP8X4),
-                                rhs_scale=h_sc[a, j0][:], start=start, stop=stop)
+        def readout_pass(o_ps, n, a, j0, cols, start, stop):
+            rows = slice(n * P, (n + 1) * P)
+            nc.tensor.matmul_mx(out=o_ps, lhsT=wread_w[:, a, rows].bitcast(FP8X4),
+                                lhsT_scale=wread_sc[WREAD_ROW:P, a, rows], rhs=h_w[a, j0][:, cols].bitcast(FP8X4),
+                                rhs_scale=h_sc[a, j0][:, cols], start=start, stop=stop)
 
-        for a in range(2):
-            prepare_winh(a)
-        for a in range(2):
-            for t in range(PACK):
-                inhibitor(a, t)
+        prepare_winh(0)
+        for t in range(PACK):
+            inhibitor(0, t, bank(t, [P, S]))
+        order_wsub_scales(0, "tab2_sc")
         nc.vector.tensor_copy(v_w[0][:], tab_w[0][:].bitcast(U32).indirect(lists[:]))
-        prepare_wsub(0)
-        a_ps = [bank(t, [P, S]) for t in range(PACK)]
+        order_wsub_words(0)
+        order_wsub_scales(1, "winh_bf0")
+        a_ps = [bank(PACK + t, [P, S]) for t in range(PACK)]
         for t in range(PACK):
             substrate_pass(a_ps[t], 0, t, 0)
         nc.vector.tensor_copy(v_w[1][:], tab_w[1][:].bitcast(U32).indirect(lists[:]))
-        prepare_wsub(1)
+        order_wsub_words(1)
         for t in range(PACK):
             substrate_pass(a_ps[t], 0, t, 1)
-            quotient(0, t, a_ps[t], False)
+            nc.scalar.activation(sub[0][:, t, :], a_ps[t][:], ACT.Square)
+            add_squares(0, t)
+            factors_on_both(0, t, slice(0, S))
+        prepare_winh(1)
+        for t in range(PACK):
+            inhibitor(1, t, bank(PACK + t, [P, S]))
+        for t in range(PACK):
+            a_ps = bank(t, [P, S])
+            for g in range(2):
+                substrate_pass(a_ps, 1, t, g)
+            nc.scalar.activation(sub[1][:, t, :], a_ps[:], ACT.Square)
         halves = [rates(0, j0, HALF) for j0 in (0, HALF)]
         for u in range(2):
             quantize_rates(0, u * HALF, HALF, halves[u])
         for t in range(PACK):
-            a_ps = bank(PACK + t, [P, S])
-            for g in range(2):
-                substrate_pass(a_ps, 1, t, g)
-            quotient(1, t, a_ps, t >= 2)
-        early = [bank(PACK + n, [P, HALF]) for n in range(4)]
-        late = [bank(n, [P, HALF]) for n in range(4)]
+            add_squares(1, t)
+        for t in range(PACK):
+            factors_on_both(1, t, slice(0, HALF))
+        for t in range(PACK):
+            factors_on_scalar(1, t, slice(HALF, S))
+
+        early = [bank(n, [P, HALF]) for n in range(4)]
+        late = [[bank(PACK + 2 * u + w, [P, 2, P]) for w in range(2)] for u in range(2)]
         for n in range(4):
-            readout_pass(late[n][:], n, 0, HALF, True, False)
-        for n in range(4):
-            readout_pass(early[n][:], n, 0, 0, True, False)
+            readout_pass(early[n][:], n, 0, 0, slice(0, HALF), True, False)
+        for u in range(2):
+            for n in range(4):
+                readout_pass(late[u][n // 2][:, n % 2, :], n, 0, HALF, slice(u * P, (u + 1) * P), n % 2 == 0, False)
+        out_rows = out.rearrange("(n p) j -> p n j", p=P)
         h_early = rates(1, 0, HALF)
-        h_next = rates(1, HALF, P)
         quantize_rates(1, 0, HALF, h_early)
-        h_last = rates(1, HALF + P, P)
+        h_late = [rates(1, HALF + u * P, P) for u in range(2)]
+        first = held([P, 4, HALF], F32, "first")
         for n in range(4):
-            readout_pass(early[n][:], n, 1, 0, False, True)
-            result = held([P, HALF], F32, "first%d" % n)
-            nc.scalar.copy(result[:], early[n][:])
-            nc.sync.dma_start(out[n * P : (n + 1) * P, :HALF], result[:])
-        quantize_rates(1, HALF, P, h_next)
-        for n in range(4):
-            readout_pass(late[n][:, :P], n, 1, HALF, False, False)
-        quantize_rates(1, HALF + P, P, h_last)
-        for n in range(4):
-            readout_pass(late[n][:, P:], n, 1, HALF + P, False, True)
-            result = held([P, HALF], F32, "last%d" % n)
+            readout_pass(early[n][:], n, 1, 0, slice(0, HALF), False, True)
+            nc.scalar.copy(first[:, n, :], early[n][:])
             if n % 2:
-                nc.vector.tensor_copy(result[:], late[n][:])
-            else:
-                nc.scalar.copy(result[:], late[n][:])
-            nc.sync.dma_start(out[n * P : (n + 1) * P, HALF:], result[:])
+                nc.sync.dma_start(out_rows[:, n - 1 : n + 1, :HALF], first[:, n - 1 : n + 1, :])
+        for u in range(2):
+            j0 = HALF + u * P
+            quantize_rates(1, j0, P, h_late[u])
+            for n in range(4):
+                readout_pass(late[u][n // 2][:, n % 2, :], n, 1, j0, slice(0, P), False, n % 2 == 1)
+            for w in range(2):
+                result = held([P, 2, P], F32, "last%d%d" % (u, w))
+                copy = nc.vector.tensor_copy if (u, w) == (1, 1) else nc.scalar.copy
+                copy(result[:], late[u][w][:])
+                nc.sync.dma_start(out_rows[:, 2 * w : 2 * w + 2, j0 : j0 + P], result[:])

@@ -54,30 +54,35 @@ def tile_list_competitive_inhibitor_assay_kernel(
         nc.vector.memset(tab_sc[:].bitcast(I32), 0)
         nc.vector.memset(tab2_sc[:].bitcast(I32), 0)
         nc.vector.memset(seed[:], 1.0)
-        nc.vector.memset(v_sc[:].bitcast(I32), 0)
-        nc.gpsimd.memset(wsub_sc[:].bitcast(I32), 0)
-        nc.gpsimd.memset(wread_sc[:].bitcast(I32), 0)
+        nc.vector.memset(wsub_sc[:].bitcast(I32), 0)
+        nc.vector.memset(v_sc[:, 1, :].bitcast(I32), 0)
+        nc.vector.memset(wread_sc[:].bitcast(I32), 0)
 
-        def load_scale_rows(queue, dst, src, first):
-            for d in range(QUADS):
-                queue.dma_start(dst[32 * d + first : 32 * d + first + 4],
-                                src[:, 4 * d : 4 * d + 4, :].rearrange("a q c -> q a c"))
+        def load_scale_rows(dst, src, first, d):
+            nc.sync.dma_start(dst.bitcast(I32)[32 * d + first : 32 * d + first + 4],
+                              src.bitcast(I32)[:, 4 * d : 4 * d + 4, :].rearrange("a q c -> q a c"))
+
+        def load_tab_scales():
+            nc.sync.dma_start(tab_sc[0:P:4].bitcast(I32), tab_scales.bitcast(I32).rearrange("a q c -> q a c"))
+
+        def load_tab(g, c0, c1):
+            nc.sync.dma_start(tab_w[g][:, c0:c1], words(tab_words[g])[:, c0:c1])
 
         def words(src):
             return src.rearrange("p t i -> p (t i)").bitcast(I32)
 
         winh_rows = winh.rearrange("(p j) c -> p j c", j=PACK)
         rate = held([P, 2, PACK], F32, "rate")
-        winh_raw = {}
+        winh_raw = [[held([P, PACK, PASS // 2], F32, "winh_raw%d%d" % (a, u)) for u in range(2)] for a in range(2)]
         wsub_raw = [held([P, 2, 2 * PASS], U8, "wsub_raw%d" % a) for a in range(2)]
         tab2_w = held([P, T2], I32, "tab2_w")
         tab_w = [held([P, T], I32, "tab_w%d" % g) for g in range(2)]
         wread_w = held([P, 2, N], I32, "wread_w")
 
-        def load_winh(a, u):
-            c0 = a * PASS + u * PASS // 2
-            winh_raw[a, u] = held([P, PACK, PASS // 2], F32, "winh_raw%d%d" % (a, u))
-            nc.sync.dma_start(winh_raw[a, u][:], winh_rows[:, :, c0 : c0 + PASS // 2])
+        def load_winh(a, u0, u1):
+            for u in range(u0 // 2, u1 // 2):
+                c0 = a * PASS + u * PASS // 2
+                nc.sync.dma_start(winh_raw[a][u][:], winh_rows[:, :, c0 : c0 + PASS // 2])
 
         def load_wsub(a):
             nc.sync.dma_start(wsub_raw[a][:].bitcast(I32),
@@ -85,38 +90,48 @@ def tile_list_competitive_inhibitor_assay_kernel(
 
         picked_sc = held([P, S], U8, "picked_sc")
 
-        def move_scales(g):
-            for i in range(4):
-                nc.sync.dma_start(v_sc[i:P:32, g, :].bitcast(I32), picked_sc[8 * i + 4 * g : P : 32].bitcast(I32))
-
-        nc.sync.dma_start(lists[:], offs)
-        nc.sync.dma_start(list2[:], offs2)
-        for g in range(2):
-            nc.scalar.dma_start(tab_sc[4 * g : P : 8].bitcast(I32), tab_scales[g].bitcast(I32))
-        load_scale_rows(nc.scalar, tab2_sc[:].bitcast(I32).rearrange("p (a c) -> p a c", a=1),
-                        tab2_scales.bitcast(I32), TAB2_ROW)
-        nc.scalar.activation(one[:], seed[:], ACT.Abs_reciprocal_sqrt)
-        load_scale_rows(nc.gpsimd, wsub_sc[:].bitcast(I32), wsub_scales.bitcast(I32), 0)
-        nc.gpsimd.dma_start(rate[:], vmax.rearrange("(a p t) -> p a t", a=2, t=PACK))
-        load_scale_rows(nc.gpsimd, wread_sc[:].bitcast(I32), wread_scales.bitcast(I32), WREAD_ROW)
-        nc.sync.dma_start(tab2_w[:], words(tab2_words[0]))
-        load_winh(0, 0)
-        load_winh(0, 1)
-        nc.sync.dma_start(tab_w[0][:], words(tab_words[0]))
+        def move_scales(g, i):
+            nc.sync.dma_start(v_sc[i:P:32, g, :].bitcast(I32), picked_sc[8 * i + 4 * g : P : 32].bitcast(I32))
 
         v2_w = held([P, S], U32, "v2_w")
         v2_sc = held([P, S], U8, "v2_sc")
         v_w = [held([P, S], U32, "v_w%d" % g) for g in range(2)]
+        tab2_rows = tab2_sc[:].rearrange("p (a c) -> p a c", a=1)
+        nc.scalar.activation(one[:], seed[:], ACT.Abs_reciprocal_sqrt)
+        nc.sync.dma_start(lists[:], offs)
+        nc.sync.dma_start(list2[:], offs2)
+        nc.sync.dma_start(tab2_w[:], words(tab2_words[0]))
+        load_tab_scales()
         nc.vector.tensor_copy(picked_sc[:], tab_sc[:].indirect(lists[:]))
-        move_scales(0)
+        nc.vector.tensor_copy(v_sc[:, 0, :].bitcast(I32), picked_sc[:].bitcast(I32))
+        load_winh(0, 0, 2)
+        load_scale_rows(tab2_rows, tab2_scales, TAB2_ROW, 0)
+        load_scale_rows(tab2_rows, tab2_scales, TAB2_ROW, 1)
+        load_scale_rows(tab2_rows, tab2_scales, TAB2_ROW, 2)
+        load_scale_rows(tab2_rows, tab2_scales, TAB2_ROW, 3)
+        load_winh(0, 2, PACK)
+        load_tab(0, 0, T)
+        load_scale_rows(wsub_sc[:], wsub_scales, 0, 0)
+        load_scale_rows(wsub_sc[:], wsub_scales, 0, 1)
+        load_scale_rows(wsub_sc[:], wsub_scales, 0, 2)
+        load_scale_rows(wsub_sc[:], wsub_scales, 0, 3)
+        move_scales(0, 1)
         load_wsub(0)
-        nc.sync.dma_start(tab_w[1][:], words(tab_words[1]))
-        move_scales(1)
+        load_tab(1, 0, T)
+        move_scales(0, 2)
+        move_scales(0, 3)
+        move_scales(1, 0)
+        move_scales(1, 1)
+        move_scales(1, 2)
+        move_scales(1, 3)
         load_wsub(1)
-        load_winh(1, 0)
-        load_winh(1, 1)
+        load_winh(1, 0, PACK)
+        nc.sync.dma_start(rate[:], vmax.rearrange("(a p t) -> p a t", a=2, t=PACK))
         nc.sync.dma_start(wread_w[:], wread_words.rearrange("g p c i -> p g (c i)").bitcast(I32))
-
+        load_scale_rows(wread_sc[:], wread_scales, WREAD_ROW, 0)
+        load_scale_rows(wread_sc[:], wread_scales, WREAD_ROW, 1)
+        load_scale_rows(wread_sc[:], wread_scales, WREAD_ROW, 2)
+        load_scale_rows(wread_sc[:], wread_scales, WREAD_ROW, 3)
         nc.vector.tensor_copy(v2_w[:], tab2_w[:].bitcast(U32).indirect(list2[:]))
         nc.vector.tensor_copy(v2_sc[:], tab2_sc[:].indirect(list2[:]))
 
@@ -127,7 +142,7 @@ def tile_list_competitive_inhibitor_assay_kernel(
             for u in range(2):
                 cast = nc.vector.tensor_copy if (a, u) == (1, 1) else nc.scalar.copy
                 cast(grouped[:, :, u * P // 2 : (u + 1) * P // 2, :].rearrange("p t m j -> p m j t"),
-                     winh_raw[a, u][:].rearrange("p j (m t) -> p m j t", t=PACK))
+                     winh_raw[a][u][:].rearrange("p j (m t) -> p m j t", t=PACK))
             codes = held([P, PASS], U32, "winh_w%d" % a)
             scales = held([P, PASS], U8, "winh_sc%d" % a)
             nc.vector.quantize_mx(out=codes[:].bitcast(FP8X4), scales=scales[:],
@@ -167,8 +182,18 @@ def tile_list_competitive_inhibitor_assay_kernel(
                                 rhs=v_w[g][:].bitcast(FP8X4), rhs_scale=v_sc[:, g, :],
                                 start=(g == 0), stop=(g == 1))
 
-        def add_squares(a, t):
-            nc.vector.tensor_tensor(total[a][:, t, :], sub[a][:, t, :], inh[a][:, t, :], ALU.add)
+        def add_squares(a, t, cols=slice(0, S)):
+            nc.vector.tensor_tensor(total[a][:, t, cols], sub[a][:, t, cols], inh[a][:, t, cols], ALU.add)
+
+        def inverse_root(dst, a, t, cols):
+            nc.scalar.activation(dst, total[a][:, t, cols], ACT.Abs_reciprocal_sqrt, bias=one[:])
+
+        def left_on_vector(a, t, cols):
+            nc.vector.scalar_tensor_tensor(left[a][:, t, cols], sub[a][:, t, cols], rate[:, a, t : t + 1],
+                                           right[a][:, t, cols], ALU.mult, ALU.mult)
+
+        def left_on_scalar(a, t, cols):
+            nc.scalar.activation(left[a][:, t, cols], sub[a][:, t, cols], ACT.Copy, scale=rate[:, a, t : t + 1])
 
         def factors_on_both(a, t, cols):
             nc.scalar.activation(right[a][:, t, cols], total[a][:, t, cols], ACT.Abs_reciprocal_sqrt, bias=one[:])
@@ -200,58 +225,64 @@ def tile_list_competitive_inhibitor_assay_kernel(
                                 lhsT_scale=wread_sc[WREAD_ROW:P, a, rows], rhs=h_w[a, j0][:, cols].bitcast(FP8X4),
                                 rhs_scale=h_sc[a, j0][:, cols], start=start, stop=stop)
 
+        full, front, back = slice(0, S), slice(0, HALF), slice(HALF, S)
         prepare_winh(0)
         for t in range(PACK):
             inhibitor(0, t, bank(t, [P, S]))
-        order_wsub_scales(0, "tab2_sc")
+        order_wsub_scales(0, None)
         nc.vector.tensor_copy(v_w[0][:], tab_w[0][:].bitcast(U32).indirect(lists[:]))
         order_wsub_words(0)
-        order_wsub_scales(1, "winh_bf0")
         a_ps = [bank(PACK + t, [P, S]) for t in range(PACK)]
         for t in range(PACK):
             substrate_pass(a_ps[t], 0, t, 0)
         nc.vector.tensor_copy(v_w[1][:], tab_w[1][:].bitcast(U32).indirect(lists[:]))
         order_wsub_words(1)
+        order_wsub_scales(1, "tab_w1")
         for t in range(PACK):
             substrate_pass(a_ps[t], 0, t, 1)
             nc.scalar.activation(sub[0][:, t, :], a_ps[t][:], ACT.Square)
-            add_squares(0, t)
-            factors_on_both(0, t, slice(0, S))
         prepare_winh(1)
         for t in range(PACK):
-            inhibitor(1, t, bank(PACK + t, [P, S]))
+            add_squares(0, t)
+            inverse_root(right[0][:, t, :], 0, t, full)
         for t in range(PACK):
+            inhibitor(1, t, bank(PACK + t, [P, S]))
             a_ps = bank(t, [P, S])
             for g in range(2):
                 substrate_pass(a_ps, 1, t, g)
             nc.scalar.activation(sub[1][:, t, :], a_ps[:], ACT.Square)
-        halves = [rates(0, j0, HALF) for j0 in (0, HALF)]
-        for u in range(2):
-            quantize_rates(0, u * HALF, HALF, halves[u])
         for t in range(PACK):
             add_squares(1, t)
         for t in range(PACK):
-            factors_on_both(1, t, slice(0, HALF))
+            left_on_vector(0, t, full)
         for t in range(PACK):
-            factors_on_scalar(1, t, slice(HALF, S))
+            inverse_root(right[1][:, t, front], 1, t, front)
+        for t in range(PACK):
+            left_on_vector(1, t, front)
+        inverse_root(root[:], 1, slice(0, 4), back)
+        nc.scalar.activation(right[1][:, :, back], root[:], ACT.Square)
+        for t in range(PACK):
+            left_on_scalar(1, t, back)
 
         early = [bank(n, [P, HALF]) for n in range(4)]
         late = [[bank(PACK + 2 * u + w, [P, 2, P]) for w in range(2)] for u in range(2)]
-        for n in range(4):
-            readout_pass(early[n][:], n, 0, 0, slice(0, HALF), True, False)
-        for u in range(2):
-            for n in range(4):
-                readout_pass(late[u][n // 2][:, n % 2, :], n, 0, HALF, slice(u * P, (u + 1) * P), n % 2 == 0, False)
         out_rows = out.rearrange("(n p) j -> p n j", p=P)
-        h_early = rates(1, 0, HALF)
-        quantize_rates(1, 0, HALF, h_early)
-        h_late = [rates(1, HALF + u * P, P) for u in range(2)]
+        fronts = [rates(a, 0, HALF) for a in range(2)]
+        for a in range(2):
+            quantize_rates(a, 0, HALF, fronts[a])
+            for n in range(4):
+                readout_pass(early[n][:], n, a, 0, slice(0, HALF), a == 0, a == 1)
+
         first = held([P, 4, HALF], F32, "first")
         for n in range(4):
-            readout_pass(early[n][:], n, 1, 0, slice(0, HALF), False, True)
             nc.scalar.copy(first[:, n, :], early[n][:])
             if n % 2:
                 nc.sync.dma_start(out_rows[:, n - 1 : n + 1, :HALF], first[:, n - 1 : n + 1, :])
+        quantize_rates(0, HALF, HALF, rates(0, HALF, HALF))
+        for u in range(2):
+            for n in range(4):
+                readout_pass(late[u][n // 2][:, n % 2, :], n, 0, HALF, slice(u * P, (u + 1) * P), n % 2 == 0, False)
+        h_late = [rates(1, HALF + u * P, P) for u in range(2)]
         for u in range(2):
             j0 = HALF + u * P
             quantize_rates(1, j0, P, h_late[u])

@@ -152,14 +152,14 @@ def tile_list_competitive_inhibitor_assay_kernel(
 
         def order_wsub_scales(a, home):
             scales = held([P, 2, PASS], U8, "wsub_s%d" % a, home)
-            nc.vector.tensor_copy(scales[:].rearrange("p g (t m) -> p g m t", t=PACK),
-                                  wsub_sc[:, :, a * PASS : (a + 1) * PASS].rearrange("p g (m t) -> p g m t", t=PACK))
+            nc.vector.tensor_copy(scales[:].rearrange("p g (t m) -> p g t m", t=PACK),
+                                  wsub_sc[:, :, a * PASS : (a + 1) * PASS].rearrange("p g (m t) -> p g t m", t=PACK))
             wsub_s.append(scales)
 
         def order_wsub_words(a):
             codes = held([P, 2, 2 * PASS], U8, "wsub_w%d" % a)
-            nc.vector.tensor_copy(codes[:].bitcast(U16).rearrange("p g (t m) -> p g m t", t=PACK),
-                                  wsub_raw[a][:].bitcast(U16).rearrange("p g (m t) -> p g m t", t=PACK))
+            nc.vector.tensor_copy(codes[:].bitcast(U16).rearrange("p g (t m) -> p g t m", t=PACK),
+                                  wsub_raw[a][:].bitcast(U16).rearrange("p g (m t) -> p g t m", t=PACK))
             wsub_w.append(codes)
 
         inh = [held([P, PACK, S], F32, "inh%d" % a) for a in range(2)]

@@ -73,16 +73,14 @@ def tile_list_competitive_inhibitor_assay_kernel(
 
         winh_rows = winh.rearrange("(p j) c -> p j c", j=PACK)
         rate = held([P, 2, PACK], F32, "rate")
-        winh_raw = [[held([P, PACK, PASS // 2], F32, "winh_raw%d%d" % (a, u)) for u in range(2)] for a in range(2)]
+        winh_raw = [held([P, PACK, PASS], F32, "winh_raw%d" % a) for a in range(2)]
         wsub_raw = [held([P, 2, 2 * PASS], U8, "wsub_raw%d" % a) for a in range(2)]
         tab2_w = held([P, T2], I32, "tab2_w")
         tab_w = [held([P, T], I32, "tab_w%d" % g) for g in range(2)]
         wread_w = held([P, 2, N], I32, "wread_w")
 
-        def load_winh(a, u0, u1):
-            for u in range(u0 // 2, u1 // 2):
-                c0 = a * PASS + u * PASS // 2
-                nc.sync.dma_start(winh_raw[a][u][:], winh_rows[:, :, c0 : c0 + PASS // 2])
+        def load_winh(a, j0, j1):
+            nc.sync.dma_start(winh_raw[a][:, j0:j1, :], winh_rows[:, j0:j1, a * PASS : (a + 1) * PASS])
 
         def load_wsub(a):
             nc.sync.dma_start(wsub_raw[a][:].bitcast(I32),
@@ -110,16 +108,17 @@ def tile_list_competitive_inhibitor_assay_kernel(
         load_scale_rows(tab2_rows, tab2_scales, TAB2_ROW, 2)
         load_scale_rows(tab2_rows, tab2_scales, TAB2_ROW, 3)
         load_winh(0, 2, PACK)
-        load_tab(0, 0, T)
+        load_tab(0, 0, T // 2)
         load_scale_rows(wsub_sc[:], wsub_scales, 0, 0)
         load_scale_rows(wsub_sc[:], wsub_scales, 0, 1)
+        load_tab(0, T // 2, T)
+        load_wsub(0)
         load_scale_rows(wsub_sc[:], wsub_scales, 0, 2)
         load_scale_rows(wsub_sc[:], wsub_scales, 0, 3)
         move_scales(0, 1)
-        load_wsub(0)
-        load_tab(1, 0, T)
         move_scales(0, 2)
         move_scales(0, 3)
+        load_tab(1, 0, T)
         move_scales(1, 0)
         move_scales(1, 1)
         move_scales(1, 2)
@@ -137,12 +136,11 @@ def tile_list_competitive_inhibitor_assay_kernel(
 
         winh_w, winh_sc, wsub_w, wsub_s = [], [], [], []
 
-        def prepare_winh(a):
+        def prepare_winh(a, shares):
             grouped = held([P, PACK, P, PACK], BF16, "winh_bf%d" % a)
-            for u in range(2):
-                cast = nc.vector.tensor_copy if (a, u) == (1, 1) else nc.scalar.copy
-                cast(grouped[:, :, u * P // 2 : (u + 1) * P // 2, :].rearrange("p t m j -> p m j t"),
-                     winh_raw[a][u][:].rearrange("p j (m t) -> p m j t", t=PACK))
+            for cast, ms, js in shares:
+                cast(grouped[:, :, ms, js].rearrange("p t m j -> p m j t"),
+                     winh_raw[a][:, js, PACK * ms.start : PACK * ms.stop].rearrange("p j (m t) -> p m j t", t=PACK))
             codes = held([P, PASS], U32, "winh_w%d" % a)
             scales = held([P, PASS], U8, "winh_sc%d" % a)
             nc.vector.quantize_mx(out=codes[:].bitcast(FP8X4), scales=scales[:],
@@ -175,6 +173,11 @@ def tile_list_competitive_inhibitor_assay_kernel(
             nc.tensor.matmul_mx(out=b_ps[:], lhsT=winh_w[a][:, cols].bitcast(FP8X4), lhsT_scale=winh_sc[a][:, cols],
                                 rhs=v2_w[:].bitcast(FP8X4), rhs_scale=v2_sc[TAB2_ROW:P], start=True, stop=True)
             nc.scalar.activation(inh[a][:, t, :], b_ps[:], ACT.Square)
+
+        def inhibitor_pass(a, t, b_ps):
+            cols = slice(t * P, (t + 1) * P)
+            nc.tensor.matmul_mx(out=b_ps[:], lhsT=winh_w[a][:, cols].bitcast(FP8X4), lhsT_scale=winh_sc[a][:, cols],
+                                rhs=v2_w[:].bitcast(FP8X4), rhs_scale=v2_sc[TAB2_ROW:P], start=True, stop=True)
 
         def substrate_pass(a_ps, a, t, g):
             nc.tensor.matmul_mx(out=a_ps[:], lhsT=wsub_w[a][:, g, 2 * t * P : 2 * (t + 1) * P].bitcast(FP4X4),
@@ -225,8 +228,8 @@ def tile_list_competitive_inhibitor_assay_kernel(
                                 lhsT_scale=wread_sc[WREAD_ROW:P, a, rows], rhs=h_w[a, j0][:, cols].bitcast(FP8X4),
                                 rhs_scale=h_sc[a, j0][:, cols], start=start, stop=stop)
 
-        full, front, back = slice(0, S), slice(0, HALF), slice(HALF, S)
-        prepare_winh(0)
+        full, front = slice(0, S), slice(0, HALF)
+        prepare_winh(0, [(nc.scalar.copy, slice(0, P), slice(0, 2)), (nc.scalar.copy, slice(0, P), slice(2, 4))])
         for t in range(PACK):
             inhibitor(0, t, bank(t, [P, S]))
         order_wsub_scales(0, None)
@@ -241,53 +244,62 @@ def tile_list_competitive_inhibitor_assay_kernel(
         for t in range(PACK):
             substrate_pass(a_ps[t], 0, t, 1)
             nc.scalar.activation(sub[0][:, t, :], a_ps[t][:], ACT.Square)
-        prepare_winh(1)
+        prepare_winh(1, [(nc.scalar.copy, slice(0, 16), slice(0, 4)), (nc.vector.tensor_copy, slice(16, P), slice(0, 4))])
         for t in range(PACK):
             add_squares(0, t)
             inverse_root(right[0][:, t, :], 0, t, full)
+        b_ps = [bank(PACK + t, [P, S]) for t in range(PACK)]
+        a_ps = [bank(t, [P, S]) for t in range(PACK)]
         for t in range(PACK):
-            inhibitor(1, t, bank(PACK + t, [P, S]))
-            a_ps = bank(t, [P, S])
+            inhibitor_pass(1, t, b_ps[t])
             for g in range(2):
-                substrate_pass(a_ps, 1, t, g)
-            nc.scalar.activation(sub[1][:, t, :], a_ps[:], ACT.Square)
+                substrate_pass(a_ps[t], 1, t, g)
+        back, every = slice(HALF, S), slice(0, PACK)
         for t in range(PACK):
-            add_squares(1, t)
+            nc.scalar.activation(sub[1][:, t, :], a_ps[t][:], ACT.Square)
+        for t in range(PACK):
+            nc.scalar.activation(inh[1][:, t, front], b_ps[t][:, front], ACT.Square)
+        for t in (slice(0, 2), slice(2, 4)):
+            add_squares(1, t, front)
+            inverse_root(right[1][:, t, front], 1, t, front)
         for t in range(PACK):
             left_on_vector(0, t, full)
         for t in range(PACK):
-            inverse_root(right[1][:, t, front], 1, t, front)
-        for t in range(PACK):
             left_on_vector(1, t, front)
-        inverse_root(root[:], 1, slice(0, 4), back)
-        nc.scalar.activation(right[1][:, :, back], root[:], ACT.Square)
+        front_first = rates(0, 0, HALF)
         for t in range(PACK):
-            left_on_scalar(1, t, back)
+            nc.scalar.activation(inh[1][:, t, back], b_ps[t][:, back], ACT.Square)
+        for t in (slice(0, 2), slice(2, 4)):
+            add_squares(1, t, back)
+        quantize_rates(0, 0, HALF, front_first)
 
+        every = slice(0, PACK)
         early = [bank(n, [P, HALF]) for n in range(4)]
         late = [[bank(PACK + 2 * u + w, [P, 2, P]) for w in range(2)] for u in range(2)]
         out_rows = out.rearrange("(n p) j -> p n j", p=P)
-        fronts = [rates(a, 0, HALF) for a in range(2)]
+        quantize_rates(1, 0, HALF, rates(1, 0, HALF))
         for a in range(2):
-            quantize_rates(a, 0, HALF, fronts[a])
             for n in range(4):
                 readout_pass(early[n][:], n, a, 0, slice(0, HALF), a == 0, a == 1)
-
         first = held([P, 4, HALF], F32, "first")
         for n in range(4):
             nc.scalar.copy(first[:, n, :], early[n][:])
             if n % 2:
                 nc.sync.dma_start(out_rows[:, n - 1 : n + 1, :HALF], first[:, n - 1 : n + 1, :])
-        quantize_rates(0, HALF, HALF, rates(0, HALF, HALF))
         for u in range(2):
-            for n in range(4):
-                readout_pass(late[u][n // 2][:, n % 2, :], n, 0, HALF, slice(u * P, (u + 1) * P), n % 2 == 0, False)
-        h_late = [rates(1, HALF + u * P, P) for u in range(2)]
+            cols = slice(HALF + u * P, HALF + (u + 1) * P)
+            inverse_root(root[:, :, u * P : (u + 1) * P], 1, every, cols)
+            nc.scalar.activation(right[1][:, :, cols], root[:, :, u * P : (u + 1) * P], ACT.Square)
+        for t in range(PACK):
+            left_on_scalar(1, t, slice(HALF, S))
         for u in range(2):
             j0 = HALF + u * P
-            quantize_rates(1, j0, P, h_late[u])
-            for n in range(4):
-                readout_pass(late[u][n // 2][:, n % 2, :], n, 1, j0, slice(0, P), False, n % 2 == 1)
+            pieces = [rates(a, j0, P) for a in range(2)]
+            for a in range(2):
+                quantize_rates(a, j0, P, pieces[a])
+                for n in range(4):
+                    readout_pass(late[u][n // 2][:, n % 2, :], n, a, j0, slice(0, P),
+                                 a == 0 and n % 2 == 0, a == 1 and n % 2 == 1)
             for w in range(2):
                 result = held([P, 2, P], F32, "last%d%d" % (u, w))
                 copy = nc.vector.tensor_copy if (u, w) == (1, 1) else nc.scalar.copy

@@ -1,6 +1,7 @@
 from contextlib import ExitStack
 
 import concourse.mybir as mybir
+from concourse.masks import make_identity
 
 K, K2, H, N, T, T2, S = 1024, 512, 1024, 512, 2048, 1024, 512
 FLOPS = 2 * S * (K * H + K2 * H + H * N)
@@ -19,8 +20,9 @@ ALU = mybir.AluOpType
 P = 128
 PACK = 4
 PASS = P * PACK
-QUADS = 4
 HALF = S // 2
+WSUB_AT = S
+PLANE_BYTES = WSUB_AT + 2 * H
 TAB2_ROW = 4
 WREAD_ROW = 8
 
@@ -37,271 +39,308 @@ def tile_list_competitive_inhibitor_assay_kernel(
         def bank(i, shape):
             return psum.tile(shape, F32, name="bank%d" % i)
 
-        def held(shape, dtype, name, tag=None):
-            return keep.tile(shape, dtype, name=name, tag=tag or name, align_bytes=64)
+        def held(shape, dtype, name):
+            return keep.tile(shape, dtype, name=name, align_bytes=64)
 
         lists = keep.tile([P, S // 16], U16, name="lists")
         list2 = keep.tile([P, S // 16], U16, name="list2")
 
         seed = held([P, 1], F32, "seed")
         one = held([P, 1], F32, "one")
+        identity = held([P, P], F32, "identity")
 
         tab_sc = held([P, T], U8, "tab_sc")
-        tab2_sc = held([P, T2], U8, "tab2_sc")
-        wsub_sc = held([P, 2, H], U8, "wsub_sc")
+        tab2_sc = held([P, 1, T2], U8, "tab2_sc")
         wread_sc = held([P, 2, N], U8, "wread_sc")
-        v_sc = held([P, 2, S], U8, "v_sc")
+        planes = held([P, PLANE_BYTES], U8, "planes")
+        planes_b = held([P, S], U8, "planes_b")
         nc.vector.memset(tab_sc[:].bitcast(I32), 0)
         nc.vector.memset(tab2_sc[:].bitcast(I32), 0)
         nc.vector.memset(seed[:], 1.0)
-        nc.vector.memset(wsub_sc[:].bitcast(I32), 0)
-        nc.vector.memset(v_sc[:, 1, :].bitcast(I32), 0)
+        nc.vector.memset(planes[:, WSUB_AT:].bitcast(I32), 0)
+        nc.vector.memset(planes_b[:].bitcast(I32), 0)
         nc.vector.memset(wread_sc[:].bitcast(I32), 0)
-
-        def load_scale_rows(dst, src, first, d):
-            nc.sync.dma_start(dst.bitcast(I32)[32 * d + first : 32 * d + first + 4],
-                              src.bitcast(I32)[:, 4 * d : 4 * d + 4, :].rearrange("a q c -> q a c"))
-
-        def load_tab_scales():
-            nc.sync.dma_start(tab_sc[0:P:4].bitcast(I32), tab_scales.bitcast(I32).rearrange("a q c -> q a c"))
-
-        def load_tab(g, c0, c1):
-            nc.sync.dma_start(tab_w[g][:, c0:c1], words(tab_words[g])[:, c0:c1])
+        nc.scalar.activation(one[:], seed[:], ACT.Abs_reciprocal_sqrt)
+        make_identity(nc, identity[:])
 
         def words(src):
             return src.rearrange("p t i -> p (t i)").bitcast(I32)
 
+        def scale_rows(src):
+            return src.bitcast(I32).rearrange("a q c -> q a c")
+
         winh_rows = winh.rearrange("(p j) c -> p j c", j=PACK)
         rate = held([P, 2, PACK], F32, "rate")
-        winh_raw = [held([P, PACK, PASS], F32, "winh_raw%d" % a) for a in range(2)]
-        wsub_raw = [held([P, 2, 2 * PASS], U8, "wsub_raw%d" % a) for a in range(2)]
+        wsub_w = held([P, 2, 2 * H], U8, "wsub_w")
         tab2_w = held([P, T2], I32, "tab2_w")
         tab_w = [held([P, T], I32, "tab_w%d" % g) for g in range(2)]
         wread_w = held([P, 2, N], I32, "wread_w")
-
-        def load_winh(a, j0, j1):
-            nc.sync.dma_start(winh_raw[a][:, j0:j1, :], winh_rows[:, j0:j1, a * PASS : (a + 1) * PASS])
-
-        def load_wsub(a):
-            nc.sync.dma_start(wsub_raw[a][:].bitcast(I32),
-                              wsub_words.bitcast(I32)[:, :, a * PASS // 2 : (a + 1) * PASS // 2].rearrange("g p c -> p g c"))
-
         picked_sc = held([P, S], U8, "picked_sc")
-
-        def move_scales(g, i):
-            nc.sync.dma_start(v_sc[i:P:32, g, :].bitcast(I32), picked_sc[8 * i + 4 * g : P : 32].bitcast(I32))
-
-        v2_w = held([P, S], U32, "v2_w")
         v2_sc = held([P, S], U8, "v2_sc")
+        winh_raw = {}
+
+        def load_winh(c0, width):
+            winh_raw[c0] = held([P, PACK, width], F32, "winh_raw%d" % c0)
+            nc.sync.dma_start(winh_raw[c0][:], winh_rows[:, :, c0 : c0 + width])
+
+        def load_tab(g, c0, c1):
+            nc.sync.dma_start(tab_w[g][:, c0:c1], words(tab_words[g])[:, c0:c1])
+
+        def close_ranks():
+            for i in range(1, 4):
+                nc.sync.dma_start(planes[i:P:32].bitcast(I32), planes[8 * i : P : 32].bitcast(I32))
+
+        def move_second_pass(rows):
+            for i in rows:
+                nc.sync.dma_start(planes_b[i:P:32].bitcast(I32), picked_sc[8 * i + 4 : P : 32].bitcast(I32))
+
         v_w = [held([P, S], U32, "v_w%d" % g) for g in range(2)]
-        tab2_rows = tab2_sc[:].rearrange("p (a c) -> p a c", a=1)
-        nc.scalar.activation(one[:], seed[:], ACT.Abs_reciprocal_sqrt)
-        nc.sync.dma_start(lists[:], offs)
-        nc.sync.dma_start(list2[:], offs2)
+        v2_w = held([P, S], U32, "v2_w")
+
+        def load_scale_rows(dst, src, first, quads):
+            for d in quads:
+                nc.sync.dma_start(dst[:].bitcast(I32)[32 * d + first : 32 * d + first + 4],
+                                  scale_rows(src)[4 * d : 4 * d + 4])
+
         nc.sync.dma_start(tab2_w[:], words(tab2_words[0]))
-        load_tab_scales()
+        nc.sync.dma_start(lists[:], offs)
+        nc.sync.dma_start(tab_sc[0:P:4].bitcast(I32), scale_rows(tab_scales))
+        nc.sync.dma_start(list2[:], offs2)
+        load_winh(0, 256)
+        load_scale_rows(tab2_sc, tab2_scales, TAB2_ROW, range(0, 2))
+        load_winh(256, 256)
+        load_scale_rows(tab2_sc, tab2_scales, TAB2_ROW, range(2, 4))
+        nc.sync.dma_start(planes[0:P:8, WSUB_AT:].bitcast(I32).rearrange("q (a c) -> q a c", a=2), scale_rows(wsub_scales))
         nc.vector.tensor_copy(picked_sc[:], tab_sc[:].indirect(lists[:]))
-        nc.vector.tensor_copy(v_sc[:, 0, :].bitcast(I32), picked_sc[:].bitcast(I32))
-        load_winh(0, 0, 2)
-        load_scale_rows(tab2_rows, tab2_scales, TAB2_ROW, 0)
-        load_scale_rows(tab2_rows, tab2_scales, TAB2_ROW, 1)
-        load_scale_rows(tab2_rows, tab2_scales, TAB2_ROW, 2)
-        load_scale_rows(tab2_rows, tab2_scales, TAB2_ROW, 3)
-        load_winh(0, 2, PACK)
-        load_tab(0, 0, T // 2)
-        load_scale_rows(wsub_sc[:], wsub_scales, 0, 0)
-        load_scale_rows(wsub_sc[:], wsub_scales, 0, 1)
-        load_tab(0, T // 2, T)
-        load_wsub(0)
-        load_scale_rows(wsub_sc[:], wsub_scales, 0, 2)
-        load_scale_rows(wsub_sc[:], wsub_scales, 0, 3)
-        move_scales(0, 1)
-        move_scales(0, 2)
-        move_scales(0, 3)
-        load_tab(1, 0, T)
-        move_scales(1, 0)
-        move_scales(1, 1)
-        move_scales(1, 2)
-        move_scales(1, 3)
-        load_wsub(1)
-        load_winh(1, 0, PACK)
+        nc.vector.tensor_copy(planes[:, :S].bitcast(I32), picked_sc[:].bitcast(I32))
+        nc.vector.tensor_copy(v2_w[:], tab2_w[:].bitcast(U32).indirect(list2[:]))
+        nc.vector.tensor_copy(v2_sc[:], tab2_sc[:, 0, :].indirect(list2[:]))
+        nc.sync.dma_start(wsub_w[:].bitcast(I32), wsub_words.bitcast(I32).rearrange("g p c -> p g c"))
+        move_second_pass(range(0, 2))
+        load_tab(0, 0, 1024)
+        close_ranks()
+        load_tab(0, 1024, 2048)
+        load_tab(1, 0, 1024)
+        move_second_pass(range(2, 4))
+        load_tab(1, 1024, 2048)
+        load_winh(512, 256)
+        load_winh(768, 256)
         nc.sync.dma_start(rate[:], vmax.rearrange("(a p t) -> p a t", a=2, t=PACK))
         nc.sync.dma_start(wread_w[:], wread_words.rearrange("g p c i -> p g (c i)").bitcast(I32))
-        load_scale_rows(wread_sc[:], wread_scales, WREAD_ROW, 0)
-        load_scale_rows(wread_sc[:], wread_scales, WREAD_ROW, 1)
-        load_scale_rows(wread_sc[:], wread_scales, WREAD_ROW, 2)
-        load_scale_rows(wread_sc[:], wread_scales, WREAD_ROW, 3)
-        nc.vector.tensor_copy(v2_w[:], tab2_w[:].bitcast(U32).indirect(list2[:]))
-        nc.vector.tensor_copy(v2_sc[:], tab2_sc[:].indirect(list2[:]))
+        load_scale_rows(wread_sc, wread_scales, WREAD_ROW, range(4))
 
-        winh_w, winh_sc, wsub_w, wsub_s = [], [], [], []
+        def gather_tab(g, u):
+            nc.vector.tensor_copy(v_w[g][:, u * HALF : (u + 1) * HALF],
+                                  tab_w[g][:].bitcast(U32).indirect(lists[:, 16 * u : 16 * (u + 1)]))
 
-        def prepare_winh(a, shares):
-            grouped = held([P, PACK, P, PACK], BF16, "winh_bf%d" % a)
-            for cast, ms, js in shares:
-                cast(grouped[:, :, ms, js].rearrange("p t m j -> p m j t"),
-                     winh_raw[a][:, js, PACK * ms.start : PACK * ms.stop].rearrange("p j (m t) -> p m j t", t=PACK))
-            codes = held([P, PASS], U32, "winh_w%d" % a)
-            scales = held([P, PASS], U8, "winh_sc%d" % a)
-            nc.vector.quantize_mx(out=codes[:].bitcast(FP8X4), scales=scales[:],
-                                  in_=grouped[:].rearrange("p t m j -> p (t m j)"))
-            winh_w.append(codes)
-            winh_sc.append(scales)
+        winh_w = [held([P, PASS], U32, "winh_w%d" % c) for c in range(2)]
+        winh_sc = [held([P, PASS], U8, "winh_sc%d" % c) for c in range(2)]
+        v_planes = (planes, planes_b)
 
-        def order_wsub_scales(a, home):
-            scales = held([P, 2, PASS], U8, "wsub_s%d" % a, home)
-            nc.vector.tensor_copy(scales[:].rearrange("p g (t m) -> p g t m", t=PACK),
-                                  wsub_sc[:, :, a * PASS : (a + 1) * PASS].rearrange("p g (m t) -> p g t m", t=PACK))
-            wsub_s.append(scales)
+        sub_t = [held([P, PACK, P], F32, "sub_t%d" % q) for q in range(4)]
+        inh_t = [held([P, PACK, P], F32, "inh_t%d" % q) for q in range(4)]
 
-        def order_wsub_words(a):
-            codes = held([P, 2, 2 * PASS], U8, "wsub_w%d" % a)
-            nc.vector.tensor_copy(codes[:].bitcast(U16).rearrange("p g (t m) -> p g t m", t=PACK),
-                                  wsub_raw[a][:].bitcast(U16).rearrange("p g (m t) -> p g t m", t=PACK))
-            wsub_w.append(codes)
+        def square(dst, src):
+            nc.scalar.activation(dst, src, ACT.Square)
 
-        inh = [held([P, PACK, S], F32, "inh%d" % a) for a in range(2)]
-        sub = [held([P, PACK, S], F32, "sub%d" % a) for a in range(2)]
-        total = [held([P, PACK, S], F32, "total%d" % a) for a in range(2)]
-        right = [held([P, PACK, S], F32, "right%d" % a) for a in range(2)]
-        left = [held([P, PACK, S], F32, "left%d" % a) for a in range(2)]
-        root = held([P, PACK, HALF], F32, "root")
-        h_w, h_sc = {}, {}
+        def inverse_root(dst, total):
+            nc.scalar.activation(dst, total, ACT.Abs_reciprocal_sqrt, bias=one[:])
 
-        def inhibitor(a, t, b_ps):
-            cols = slice(t * P, (t + 1) * P)
-            nc.tensor.matmul_mx(out=b_ps[:], lhsT=winh_w[a][:, cols].bitcast(FP8X4), lhsT_scale=winh_sc[a][:, cols],
-                                rhs=v2_w[:].bitcast(FP8X4), rhs_scale=v2_sc[TAB2_ROW:P], start=True, stop=True)
-            nc.scalar.activation(inh[a][:, t, :], b_ps[:], ACT.Square)
+        def scaled_product(dst, sub, c, t, root):
+            nc.vector.scalar_tensor_tensor(dst, sub, rate[:, c, t : t + 1], root, ALU.mult, ALU.mult)
 
-        def inhibitor_pass(a, t, b_ps):
-            cols = slice(t * P, (t + 1) * P)
-            nc.tensor.matmul_mx(out=b_ps[:], lhsT=winh_w[a][:, cols].bitcast(FP8X4), lhsT_scale=winh_sc[a][:, cols],
-                                rhs=v2_w[:].bitcast(FP8X4), rhs_scale=v2_sc[TAB2_ROW:P], start=True, stop=True)
+        def work(name):
+            return held([P, PACK, HALF], F32, name)
 
-        def substrate_pass(a_ps, a, t, g):
-            nc.tensor.matmul_mx(out=a_ps[:], lhsT=wsub_w[a][:, g, 2 * t * P : 2 * (t + 1) * P].bitcast(FP4X4),
-                                lhsT_scale=wsub_s[a][:, g, t * P : (t + 1) * P],
-                                rhs=v_w[g][:].bitcast(FP8X4), rhs_scale=v_sc[:, g, :],
-                                start=(g == 0), stop=(g == 1))
+        def turn(dst, blocks, start, stop):
+            steps = [(e, w) for e in range(2) for w in range(2)]
+            for i, (e, w) in enumerate(steps):
+                nc.tensor.matmul(dst[:, e, w * P : (w + 1) * P], blocks(e, w), identity[:],
+                                 start=(start and i == 0), stop=(stop and i == 3), is_transpose=True)
 
-        def add_squares(a, t, cols=slice(0, S)):
-            nc.vector.tensor_tensor(total[a][:, t, cols], sub[a][:, t, cols], inh[a][:, t, cols], ALU.add)
-
-        def inverse_root(dst, a, t, cols):
-            nc.scalar.activation(dst, total[a][:, t, cols], ACT.Abs_reciprocal_sqrt, bias=one[:])
-
-        def left_on_vector(a, t, cols):
-            nc.vector.scalar_tensor_tensor(left[a][:, t, cols], sub[a][:, t, cols], rate[:, a, t : t + 1],
-                                           right[a][:, t, cols], ALU.mult, ALU.mult)
-
-        def left_on_scalar(a, t, cols):
-            nc.scalar.activation(left[a][:, t, cols], sub[a][:, t, cols], ACT.Copy, scale=rate[:, a, t : t + 1])
-
-        def factors_on_both(a, t, cols):
-            nc.scalar.activation(right[a][:, t, cols], total[a][:, t, cols], ACT.Abs_reciprocal_sqrt, bias=one[:])
-            nc.vector.scalar_tensor_tensor(left[a][:, t, cols], sub[a][:, t, cols], rate[:, a, t : t + 1],
-                                           right[a][:, t, cols], ALU.mult, ALU.mult)
-
-        def factors_on_scalar(a, t, cols):
-            nc.scalar.activation(root[:, t, :], total[a][:, t, cols], ACT.Abs_reciprocal_sqrt, bias=one[:])
-            nc.scalar.activation(right[a][:, t, cols], root[:, t, :], ACT.Square)
-            nc.scalar.activation(left[a][:, t, cols], sub[a][:, t, cols], ACT.Copy, scale=rate[:, a, t : t + 1])
-
-        def rates(a, j0, width):
-            cols = slice(j0, j0 + width)
-            h_bf = held([P, width, PACK], BF16, "h_bf%d_%d" % (a, j0))
+        def rates(name, left, right):
+            h_bf = held([P, left.shape[2], PACK], BF16, name)
             nc.vector.tensor_tensor(h_bf[:].rearrange("p (c i) t -> p c t i", i=4),
-                                    left[a][:, :, cols].rearrange("p t (c i) -> p c t i", i=4),
-                                    right[a][:, :, cols].rearrange("p t (c i) -> p c t i", i=4), ALU.mult)
+                                    left.rearrange("p t (c i) -> p c t i", i=4),
+                                    right.rearrange("p t (c i) -> p c t i", i=4), ALU.mult)
             return h_bf
 
-        def quantize_rates(a, j0, width, h_bf):
-            h_w[a, j0] = held([P, width], U32, "h_w%d_%d" % (a, j0))
-            h_sc[a, j0] = held([P, width], U8, "h_sc%d_%d" % (a, j0))
-            nc.vector.quantize_mx(out=h_w[a, j0][:].bitcast(FP8X4), scales=h_sc[a, j0][:],
+        def quantize_rates(name, h_bf):
+            codes = held([P, h_bf.shape[1]], U32, name + "_w")
+            scales = held([P, h_bf.shape[1]], U8, name + "_sc")
+            nc.vector.quantize_mx(out=codes[:].bitcast(FP8X4), scales=scales[:],
                                   in_=h_bf[:].rearrange("p j t -> p (j t)"))
+            return codes, scales
 
-        def readout_pass(o_ps, n, a, j0, cols, start, stop):
-            rows = slice(n * P, (n + 1) * P)
-            nc.tensor.matmul_mx(out=o_ps, lhsT=wread_w[:, a, rows].bitcast(FP8X4),
-                                lhsT_scale=wread_sc[WREAD_ROW:P, a, rows], rhs=h_w[a, j0][:, cols].bitcast(FP8X4),
-                                rhs_scale=h_sc[a, j0][:, cols], start=start, stop=stop)
+        def readout_pass(o_ps, n, c, h, cols, start, stop):
+            nc.tensor.matmul_mx(out=o_ps, lhsT=wread_w[:, c, n * P : (n + 1) * P].bitcast(FP8X4),
+                                lhsT_scale=wread_sc[WREAD_ROW:P, c, n * P : (n + 1) * P], rhs=h[0][:, cols].bitcast(FP8X4),
+                                rhs_scale=h[1][:, cols], start=start, stop=stop)
 
-        full, front = slice(0, S), slice(0, HALF)
-        prepare_winh(0, [(nc.scalar.copy, slice(0, P), slice(0, 2)), (nc.scalar.copy, slice(0, P), slice(2, 4))])
+        whole = slice(0, HALF)
+        pairs = (slice(0, 2), slice(2, 4))
+
+        winh_bf = held([P, PACK, P, PACK], BF16, "winh_bf0")
+        for piece in range(2):
+            nc.scalar.copy(winh_bf[:, :, piece * P // 2 : (piece + 1) * P // 2, :].rearrange("p t m j -> p m j t"),
+                           winh_raw[piece * HALF][:].rearrange("p j (m t) -> p m j t", t=PACK))
+        nc.vector.quantize_mx(out=winh_w[0][:].bitcast(FP8X4), scales=winh_sc[0][:],
+                              in_=winh_bf[:].rearrange("p t m j -> p (t m j)"))
+        inh0, sub0, total0, root0, left0 = [held([P, PACK, S], F32, name)
+                                            for name in ("inh0", "sub0", "total0", "root0", "left0")]
         for t in range(PACK):
-            inhibitor(0, t, bank(t, [P, S]))
-        order_wsub_scales(0, None)
-        nc.vector.tensor_copy(v_w[0][:], tab_w[0][:].bitcast(U32).indirect(lists[:]))
-        order_wsub_words(0)
-        a_ps = [bank(PACK + t, [P, S]) for t in range(PACK)]
-        for t in range(PACK):
-            substrate_pass(a_ps[t], 0, t, 0)
-        nc.vector.tensor_copy(v_w[1][:], tab_w[1][:].bitcast(U32).indirect(lists[:]))
-        order_wsub_words(1)
-        order_wsub_scales(1, "tab_w1")
-        for t in range(PACK):
-            substrate_pass(a_ps[t], 0, t, 1)
-            nc.scalar.activation(sub[0][:, t, :], a_ps[t][:], ACT.Square)
-        prepare_winh(1, [(nc.scalar.copy, slice(0, 16), slice(0, 4)), (nc.vector.tensor_copy, slice(16, P), slice(0, 4))])
-        for t in range(PACK):
-            add_squares(0, t)
-            inverse_root(right[0][:, t, :], 0, t, full)
-        b_ps = [bank(PACK + t, [P, S]) for t in range(PACK)]
+            b_ps = bank(4 + t, [P, S])
+            cols = slice(t * P, (t + 1) * P)
+            nc.tensor.matmul_mx(out=b_ps[:], lhsT=winh_w[0][:, cols].bitcast(FP8X4), lhsT_scale=winh_sc[0][:, cols],
+                                rhs=v2_w[:].bitcast(FP8X4), rhs_scale=v2_sc[TAB2_ROW:P], start=True, stop=True)
+            square(inh0[:, t, :], b_ps[:])
+
+        wsub_s = held([P, 2, PASS], U8, "wsub_s")
+        nc.vector.tensor_copy(wsub_s[:].rearrange("p g (t m) -> p g t m", t=PACK),
+                              planes[:, WSUB_AT:].rearrange("p (g c m t) -> p c g t m", g=2, c=2, t=PACK)[:, 0])
+        wsub_o = held([P, 2, 2 * PASS], U8, "wsub_o")
+        nc.vector.tensor_copy(wsub_o[:].bitcast(U16).rearrange("p g (t m) -> p g t m", t=PACK),
+                              wsub_w[:, :, : 2 * PASS].bitcast(U16).rearrange("p g (m t) -> p g t m", t=PACK))
+
+        def substrate_pass(a_ps, t, g):
+            nc.tensor.matmul_mx(out=a_ps[:], lhsT=wsub_o[:, g, 2 * t * P : 2 * (t + 1) * P].bitcast(FP4X4),
+                                lhsT_scale=wsub_s[:, g, t * P : (t + 1) * P],
+                                rhs=v_w[g][:].bitcast(FP8X4), rhs_scale=v_planes[g][:, :S],
+                                start=(g == 0), stop=(g == 1))
+
+        def substrate_turned(a_ps, q, g):
+            first = WSUB_AT + g * H + PASS
+            nc.tensor.matmul_mx(out=a_ps[:], lhsT=v_w[g][:, q * P : (q + 1) * P].bitcast(FP8X4),
+                                lhsT_scale=v_planes[g][:, q * P : (q + 1) * P],
+                                rhs=wsub_w[:, g, 2 * PASS :].bitcast(FP4X4), rhs_scale=planes[:, first : first + PASS],
+                                start=(g == 0), stop=(g == 1))
+
+        def finish_turned(q):
+            substrate_turned(turned_ps[q], q, 1)
+            square(sub_t[q][:], turned_ps[q][:].rearrange("p (m t) -> p t m", t=PACK))
+
+        def finish_direct(t):
+            substrate_pass(a_ps[t], t, 1)
+            square(sub0[:, t, :], a_ps[t][:])
+
+        def inhibitor_turned(q, i):
+            b_ps = bank(i, [P, PASS])
+            nc.tensor.matmul_mx(out=b_ps[:], lhsT=v2_w[:, q * P : (q + 1) * P].bitcast(FP8X4),
+                                lhsT_scale=v2_sc[TAB2_ROW:P, q * P : (q + 1) * P],
+                                rhs=winh_w[1][:].bitcast(FP8X4), rhs_scale=winh_sc[1][:], start=True, stop=True)
+            square(inh_t[q][:], b_ps[:].rearrange("p (m t) -> p t m", t=PACK))
+
+        def prepare_winh_piece(piece, copy):
+            cols = slice(piece * HALF, (piece + 1) * HALF)
+            grouped = held([P, HALF, PACK], BF16, "winh_bf1%d" % piece)
+            copy(grouped[:].rearrange("p (c i) j -> p c j i", i=4),
+                 winh_raw[PASS + cols.start][:].rearrange("p j (c i) -> p c j i", i=4))
+            nc.vector.quantize_mx(out=winh_w[1][:, cols].bitcast(FP8X4), scales=winh_sc[1][:, cols],
+                                  in_=grouped[:].rearrange("p c j -> p (c j)"))
+
+        root1, left1 = [[work("%s1%d" % (name, u)) for u in range(2)] for name in ("root", "left")]
+        total_ps, sub_ps = {}, {}
+
+        def open_total(u, pair, i):
+            total_ps[u, pair] = bank(i, [P, 2, HALF])
+            turn(total_ps[u, pair], lambda e, w: sub_t[2 * u + w][:, 2 * pair + e, :], True, False)
+
+        def close_total(u, pair):
+            turn(total_ps[u, pair], lambda e, w: inh_t[2 * u + w][:, 2 * pair + e, :], False, True)
+            inverse_root(root1[u][:, pairs[pair], :], total_ps[u, pair][:])
+
+        def close_total_squared(u, pair):
+            turn(total_ps[u, pair], lambda e, w: inh_t[2 * u + w][:, 2 * pair + e, :], False, True)
+            root = held([P, 2, HALF], F32, "root_last")
+            inverse_root(root[:], total_ps[u, pair][:])
+            square(root1[u][:, pairs[pair], :], root[:])
+
+        def left_on_scalar(u, t):
+            nc.scalar.activation(left1[u][:, t, :], sub_ps[u, t // 2][:, t % 2, :], ACT.Copy, scale=rate[:, 1, t : t + 1])
+
+        def turn_sub(u, pair, i):
+            sub_ps[u, pair] = bank(i, [P, 2, HALF])
+            turn(sub_ps[u, pair], lambda e, w: sub_t[2 * u + w][:, 2 * pair + e, :], True, True)
+
+        def lefts(u, ts):
+            for t in ts:
+                scaled_product(left1[u][:, t, :], sub_ps[u, t // 2][:, t % 2, :], 1, t, root1[u][:, t, :])
+
+        def add(ts):
+            nc.vector.tensor_tensor(total0[:, ts, :], sub0[:, ts, :], inh0[:, ts, :], ALU.add)
+            inverse_root(root0[:, ts, :], total0[:, ts, :])
+
+        for u in range(2):
+            gather_tab(0, u)
         a_ps = [bank(t, [P, S]) for t in range(PACK)]
         for t in range(PACK):
-            inhibitor_pass(1, t, b_ps[t])
-            for g in range(2):
-                substrate_pass(a_ps[t], 1, t, g)
-        back, every = slice(HALF, S), slice(0, PACK)
+            substrate_pass(a_ps[t], t, 0)
+        turned_ps = [bank(4 + q, [P, PASS]) for q in range(2)]
+        for q in range(2):
+            substrate_turned(turned_ps[q], q, 0)
+        for u in range(2):
+            gather_tab(1, u)
+        finish_turned(0)
+        finish_turned(1)
+        prepare_winh_piece(0, nc.vector.tensor_copy)
+        prepare_winh_piece(1, nc.vector.tensor_copy)
         for t in range(PACK):
-            nc.scalar.activation(sub[1][:, t, :], a_ps[t][:], ACT.Square)
+            finish_direct(t)
         for t in range(PACK):
-            nc.scalar.activation(inh[1][:, t, front], b_ps[t][:, front], ACT.Square)
-        for t in (slice(0, 2), slice(2, 4)):
-            add_squares(1, t, front)
-            inverse_root(right[1][:, t, front], 1, t, front)
+            add(slice(t, t + 1))
+        for pair in range(2):
+            open_total(0, pair, pair)
         for t in range(PACK):
-            left_on_vector(0, t, full)
-        for t in range(PACK):
-            left_on_vector(1, t, front)
-        front_first = rates(0, 0, HALF)
-        for t in range(PACK):
-            nc.scalar.activation(inh[1][:, t, back], b_ps[t][:, back], ACT.Square)
-        for t in (slice(0, 2), slice(2, 4)):
-            add_squares(1, t, back)
-        quantize_rates(0, 0, HALF, front_first)
+            scaled_product(left0[:, t, :], sub0[:, t, :], 0, t, root0[:, t, :])
+        inhibitor_turned(0, 4)
+        inhibitor_turned(1, 5)
+        for pair in range(2):
+            close_total(0, pair)
+            turn_sub(0, pair, 6 + pair)
+        for q in (2, 3):
+            turned_ps.append(bank(q, [P, PASS]))
+            substrate_turned(turned_ps[q], q, 0)
+            finish_turned(q)
+        h_bf00 = rates("h_bf00", left0[:, :, :HALF], root0[:, :, :HALF])
+        h_bf01 = rates("h_bf01", left0[:, :, HALF:], root0[:, :, HALF:])
+        h00 = quantize_rates("h00", h_bf00)
+        inhibitor_turned(2, 4)
+        inhibitor_turned(3, 5)
+        open_total(1, 1, 1)
+        turn_sub(1, 1, 3)
+        close_total_squared(1, 1)
+        open_total(1, 0, 0)
+        close_total(1, 0)
+        turn_sub(1, 0, 2)
+        for t in (2, 3):
+            left_on_scalar(1, t)
+        lefts(0, range(4))
+        h01 = quantize_rates("h01", h_bf01)
+        h_bf10 = rates("h_bf10", left1[0][:], root1[0][:])
+        lefts(1, range(2))
+        h10 = quantize_rates("h10", h_bf10)
 
-        every = slice(0, PACK)
-        early = [bank(n, [P, HALF]) for n in range(4)]
-        late = [[bank(PACK + 2 * u + w, [P, 2, P]) for w in range(2)] for u in range(2)]
         out_rows = out.rearrange("(n p) j -> p n j", p=P)
-        quantize_rates(1, 0, HALF, rates(1, 0, HALF))
-        for a in range(2):
+        early = [bank(i, [P, 2, HALF]) for i in (4, 5)]
+        for w in range(2):
+            for c, h in enumerate((h00, h10)):
+                for e in range(2):
+                    readout_pass(early[w][:, e, :], 2 * w + e, c, h, whole, c == 0 and e == 0, c == 1 and e == 1)
+            first = held([P, 2, HALF], F32, "first%d" % w)
+            nc.scalar.copy(first[:], early[w][:])
+            nc.sync.dma_start(out_rows[:, 2 * w : 2 * w + 2, :HALF], first[:])
+        late = [[bank(i, [P, 2, P]) for i in row] for row in ((6, 7), (0, 1))]
+        for u in range(2):
             for n in range(4):
-                readout_pass(early[n][:], n, a, 0, slice(0, HALF), a == 0, a == 1)
-        first = held([P, 4, HALF], F32, "first")
-        for n in range(4):
-            nc.scalar.copy(first[:, n, :], early[n][:])
-            if n % 2:
-                nc.sync.dma_start(out_rows[:, n - 1 : n + 1, :HALF], first[:, n - 1 : n + 1, :])
+                readout_pass(late[u][n // 2][:, n % 2, :], n, 0, h01, slice(u * P, (u + 1) * P), n % 2 == 0, False)
+        h_late = [rates("h_bf11%d" % u, left1[1][:, :, u * P : (u + 1) * P], root1[1][:, :, u * P : (u + 1) * P])
+                  for u in range(2)]
         for u in range(2):
-            cols = slice(HALF + u * P, HALF + (u + 1) * P)
-            inverse_root(root[:, :, u * P : (u + 1) * P], 1, every, cols)
-            nc.scalar.activation(right[1][:, :, cols], root[:, :, u * P : (u + 1) * P], ACT.Square)
-        for t in range(PACK):
-            left_on_scalar(1, t, slice(HALF, S))
-        for u in range(2):
-            j0 = HALF + u * P
-            pieces = [rates(a, j0, P) for a in range(2)]
-            for a in range(2):
-                quantize_rates(a, j0, P, pieces[a])
-                for n in range(4):
-                    readout_pass(late[u][n // 2][:, n % 2, :], n, a, j0, slice(0, P),
-                                 a == 0 and n % 2 == 0, a == 1 and n % 2 == 1)
+            h = quantize_rates("h11%d" % u, h_late[u])
+            for n in range(4):
+                readout_pass(late[u][n // 2][:, n % 2, :], n, 1, h, slice(0, P), False, n % 2 == 1)
             for w in range(2):
                 result = held([P, 2, P], F32, "last%d%d" % (u, w))
                 copy = nc.vector.tensor_copy if (u, w) == (1, 1) else nc.scalar.copy
                 copy(result[:], late[u][w][:])
-                nc.sync.dma_start(out_rows[:, 2 * w : 2 * w + 2, j0 : j0 + P], result[:])
+                nc.sync.dma_start(out_rows[:, 2 * w : 2 * w + 2, HALF + u * P : HALF + (u + 1) * P], result[:])

@@ -39,8 +39,8 @@ def tile_list_competitive_inhibitor_assay_kernel(
         def bank(i, shape):
             return psum.tile(shape, F32, name="bank%d" % i)
 
-        def held(shape, dtype, name):
-            return keep.tile(shape, dtype, name=name, align_bytes=64)
+        def held(shape, dtype, name, tag=None):
+            return keep.tile(shape, dtype, name=name, tag=tag or name, align_bytes=64)
 
         lists = keep.tile([P, S // 16], U16, name="lists")
         list2 = keep.tile([P, S // 16], U16, name="list2")
@@ -60,8 +60,9 @@ def tile_list_competitive_inhibitor_assay_kernel(
         nc.vector.memset(planes[:, WSUB_AT:].bitcast(I32), 0)
         nc.vector.memset(planes_b[:].bitcast(I32), 0)
         nc.vector.memset(wread_sc[:].bitcast(I32), 0)
+        nc.vector.memset(identity[:], 0.0)
         nc.scalar.activation(one[:], seed[:], ACT.Abs_reciprocal_sqrt)
-        make_identity(nc, identity[:])
+        make_identity(nc, identity[:], nomemset=True)
 
         def words(src):
             return src.rearrange("p t i -> p (t i)").bitcast(I32)
@@ -153,7 +154,7 @@ def tile_list_competitive_inhibitor_assay_kernel(
             return held([P, PACK, HALF], F32, name)
 
         def turn(dst, blocks, start, stop):
-            steps = [(e, w) for e in range(2) for w in range(2)]
+            steps = [(e, w) for w in range(2) for e in range(2)]
             for i, (e, w) in enumerate(steps):
                 nc.tensor.matmul(dst[:, e, w * P : (w + 1) * P], blocks(e, w), identity[:],
                                  start=(start and i == 0), stop=(stop and i == 3), is_transpose=True)
@@ -186,8 +187,7 @@ def tile_list_competitive_inhibitor_assay_kernel(
                            winh_raw[piece * HALF][:].rearrange("p j (m t) -> p m j t", t=PACK))
         nc.vector.quantize_mx(out=winh_w[0][:].bitcast(FP8X4), scales=winh_sc[0][:],
                               in_=winh_bf[:].rearrange("p t m j -> p (t m j)"))
-        inh0, sub0, total0, root0, left0 = [held([P, PACK, S], F32, name)
-                                            for name in ("inh0", "sub0", "total0", "root0", "left0")]
+        inh0, sub0, root0, left0 = [held([P, PACK, S], F32, name) for name in ("inh0", "sub0", "root0", "left0")]
         for t in range(PACK):
             b_ps = bank(4 + t, [P, S])
             cols = slice(t * P, (t + 1) * P)
@@ -266,9 +266,14 @@ def tile_list_competitive_inhibitor_assay_kernel(
             for t in ts:
                 scaled_product(left1[u][:, t, :], sub_ps[u, t // 2][:, t % 2, :], 1, t, root1[u][:, t, :])
 
-        def add(ts):
-            nc.vector.tensor_tensor(total0[:, ts, :], sub0[:, ts, :], inh0[:, ts, :], ALU.add)
-            inverse_root(root0[:, ts, :], total0[:, ts, :])
+        totals = {}
+
+        def add(t, home=None):
+            totals[t] = held([P, S], F32, "total%d" % t, home)
+            nc.vector.tensor_tensor(totals[t][:], sub0[:, t, :], inh0[:, t, :], ALU.add)
+
+        def direct_root(t):
+            inverse_root(root0[:, t, :], totals[t][:])
 
         for u in range(2):
             gather_tab(0, u)
@@ -287,12 +292,15 @@ def tile_list_competitive_inhibitor_assay_kernel(
         for t in range(PACK):
             finish_direct(t)
         for t in range(PACK):
-            add(slice(t, t + 1))
+            add(t)
+        for t in range(3):
+            direct_root(t)
+        inhibitor_turned(0, 4)
+        direct_root(3)
         for pair in range(2):
             open_total(0, pair, pair)
         for t in range(PACK):
             scaled_product(left0[:, t, :], sub0[:, t, :], 0, t, root0[:, t, :])
-        inhibitor_turned(0, 4)
         inhibitor_turned(1, 5)
         for pair in range(2):
             close_total(0, pair)

@@ -258,6 +258,11 @@ def tile_list_competitive_inhibitor_assay_kernel(
         def left_on_scalar(u, t):
             nc.scalar.activation(left1[u][:, t, :], sub_ps[u, t // 2][:, t % 2, :], ACT.Copy, scale=rate[:, 1, t : t + 1])
 
+        def turn_block(dst, src, pair, w, start, stop):
+            for e in range(2):
+                nc.tensor.matmul(dst[:, e, w * P : (w + 1) * P], src[:, 2 * pair + e, :], identity[:],
+                                 start=(start and e == 0), stop=(stop and e == 1), is_transpose=True)
+
         def turn_sub(u, pair, i):
             sub_ps[u, pair] = bank(i, [P, 2, HALF])
             turn(sub_ps[u, pair], lambda e, w: sub_t[2 * u + w][:, 2 * pair + e, :], True, True)
@@ -304,21 +309,28 @@ def tile_list_competitive_inhibitor_assay_kernel(
         inhibitor_turned(1, 5)
         for pair in range(2):
             close_total(0, pair)
-            turn_sub(0, pair, 6 + pair)
-        for q in (2, 3):
-            turned_ps.append(bank(q, [P, PASS]))
-            substrate_turned(turned_ps[q], q, 0)
-            finish_turned(q)
+            turn_sub(0, pair, (6, 3)[pair])
+        turned_ps.append(bank(2, [P, PASS]))
+        substrate_turned(turned_ps[2], 2, 0)
+        finish_turned(2)
+        inhibitor_turned(2, 4)
+        turned_ps.append(bank(5, [P, PASS]))
+        substrate_turned(turned_ps[3], 3, 0)
+        finish_turned(3)
         h_bf00 = rates("h_bf00", left0[:, :, :HALF], root0[:, :, :HALF])
         h_bf01 = rates("h_bf01", left0[:, :, HALF:], root0[:, :, HALF:])
         h00 = quantize_rates("h00", h_bf00)
-        inhibitor_turned(2, 4)
-        inhibitor_turned(3, 5)
-        open_total(1, 1, 1)
-        turn_sub(1, 1, 3)
-        close_total_squared(1, 1)
-        open_total(1, 0, 0)
-        close_total(1, 0)
+        inhibitor_turned(3, 4)
+        turn_sub(1, 1, 7)
+        for pair in (1, 0):
+            total_ps[1, pair] = bank(pair, [P, 2, HALF])
+            for w in range(2):
+                turn_block(total_ps[1, pair], sub_t[2 + w], pair, w, w == 0, False)
+                turn_block(total_ps[1, pair], inh_t[2 + w], pair, w, False, w == 1)
+        root = held([P, 2, HALF], F32, "root_last")
+        inverse_root(root[:], total_ps[1, 1][:])
+        inverse_root(root1[1][:, pairs[0], :], total_ps[1, 0][:])
+        square(root1[1][:, pairs[1], :], root[:])
         turn_sub(1, 0, 2)
         for t in (2, 3):
             left_on_scalar(1, t)
@@ -329,7 +341,7 @@ def tile_list_competitive_inhibitor_assay_kernel(
         h10 = quantize_rates("h10", h_bf10)
 
         out_rows = out.rearrange("(n p) j -> p n j", p=P)
-        early = [bank(i, [P, 2, HALF]) for i in (4, 5)]
+        early = [bank(i, [P, 2, HALF]) for i in (5, 4)]
         for w in range(2):
             for c, h in enumerate((h00, h10)):
                 for e in range(2):

@@ -98,18 +98,16 @@ def tile_list_competitive_inhibitor_assay_kernel(
         v_w = [held([P, S], U32, "v_w%d" % g) for g in range(2)]
         v2_w = held([P, S], U32, "v2_w")
 
-        def load_scale_rows(dst, src, first, quads):
-            for d in quads:
-                nc.sync.dma_start(dst[:].bitcast(I32)[32 * d + first : 32 * d + first + 4],
-                                  scale_rows(src)[4 * d : 4 * d + 4])
+        def load_scale_rows(dst, src, first, rows):
+            for r in rows:
+                nc.sync.dma_start(dst[:].bitcast(I32)[first + r : P : 32], scale_rows(src)[r:16:4])
 
         nc.sync.dma_start(tab2_w[:], words(tab2_words[0]))
         nc.sync.dma_start(lists[:], offs)
         nc.sync.dma_start(tab_sc[0:P:4].bitcast(I32), scale_rows(tab_scales))
         nc.sync.dma_start(list2[:], offs2)
-        load_winh(0, 256)
         load_scale_rows(tab2_sc, tab2_scales, TAB2_ROW, range(0, 2))
-        load_winh(256, 256)
+        load_winh(0, PASS)
         load_scale_rows(tab2_sc, tab2_scales, TAB2_ROW, range(2, 4))
         nc.sync.dma_start(planes[0:P:8, WSUB_AT:].bitcast(I32).rearrange("q (a c) -> q a c", a=2), scale_rows(wsub_scales))
         nc.vector.tensor_copy(picked_sc[:], tab_sc[:].indirect(lists[:]))
@@ -138,7 +136,7 @@ def tile_list_competitive_inhibitor_assay_kernel(
         winh_sc = [held([P, PASS], U8, "winh_sc%d" % c) for c in range(2)]
         v_planes = (planes, planes_b)
 
-        sub_t = [held([P, PACK, P], F32, "sub_t%d" % q) for q in range(4)]
+        sub_t = {q: held([P, PACK, P], F32, "sub_t%d" % q) for q in (0, 2, 3)}
         inh_t = [held([P, PACK, P], F32, "inh_t%d" % q) for q in range(4)]
 
         def square(dst, src):
@@ -184,16 +182,17 @@ def tile_list_competitive_inhibitor_assay_kernel(
         winh_bf = held([P, PACK, P, PACK], BF16, "winh_bf0")
         for piece in range(2):
             nc.scalar.copy(winh_bf[:, :, piece * P // 2 : (piece + 1) * P // 2, :].rearrange("p t m j -> p m j t"),
-                           winh_raw[piece * HALF][:].rearrange("p j (m t) -> p m j t", t=PACK))
+                           winh_raw[0][:, :, piece * HALF : (piece + 1) * HALF].rearrange("p j (m t) -> p m j t", t=PACK))
         nc.vector.quantize_mx(out=winh_w[0][:].bitcast(FP8X4), scales=winh_sc[0][:],
                               in_=winh_bf[:].rearrange("p t m j -> p (t m j)"))
-        inh0, sub0, root0, left0 = [held([P, PACK, S], F32, name) for name in ("inh0", "sub0", "root0", "left0")]
+        sub0, root0, left0 = [held([P, PACK, S], F32, name) for name in ("sub0", "root0", "left0")]
+        inh0 = [held([P, S], F32, "inh0%d" % t) for t in range(PACK)]
         for t in range(PACK):
             b_ps = bank(4 + t, [P, S])
             cols = slice(t * P, (t + 1) * P)
             nc.tensor.matmul_mx(out=b_ps[:], lhsT=winh_w[0][:, cols].bitcast(FP8X4), lhsT_scale=winh_sc[0][:, cols],
                                 rhs=v2_w[:].bitcast(FP8X4), rhs_scale=v2_sc[TAB2_ROW:P], start=True, stop=True)
-            square(inh0[:, t, :], b_ps[:])
+            square(inh0[t][:], b_ps[:])
 
         wsub_s = held([P, 2, PASS], U8, "wsub_s")
         nc.vector.tensor_copy(wsub_s[:].rearrange("p g (t m) -> p g t m", t=PACK),
@@ -230,9 +229,9 @@ def tile_list_competitive_inhibitor_assay_kernel(
                                 rhs=winh_w[1][:].bitcast(FP8X4), rhs_scale=winh_sc[1][:], start=True, stop=True)
             square(inh_t[q][:], b_ps[:].rearrange("p (m t) -> p t m", t=PACK))
 
-        def prepare_winh_piece(piece, copy):
+        def prepare_winh_piece(piece, copy, home=None):
             cols = slice(piece * HALF, (piece + 1) * HALF)
-            grouped = held([P, HALF, PACK], BF16, "winh_bf1%d" % piece)
+            grouped = held([P, HALF, PACK], BF16, "winh_bf1%d" % piece, home)
             copy(grouped[:].rearrange("p (c i) j -> p c j i", i=4),
                  winh_raw[PASS + cols.start][:].rearrange("p j (c i) -> p c j i", i=4))
             nc.vector.quantize_mx(out=winh_w[1][:, cols].bitcast(FP8X4), scales=winh_sc[1][:, cols],
@@ -275,7 +274,7 @@ def tile_list_competitive_inhibitor_assay_kernel(
 
         def add(t, home=None):
             totals[t] = held([P, S], F32, "total%d" % t, home)
-            nc.vector.tensor_tensor(totals[t][:], sub0[:, t, :], inh0[:, t, :], ALU.add)
+            nc.vector.tensor_tensor(totals[t][:], sub0[:, t, :], inh0[t][:], ALU.add)
 
         def direct_root(t):
             inverse_root(root0[:, t, :], totals[t][:])
@@ -291,12 +290,14 @@ def tile_list_competitive_inhibitor_assay_kernel(
         for u in range(2):
             gather_tab(1, u)
         finish_turned(0)
-        finish_turned(1)
         prepare_winh_piece(0, nc.vector.tensor_copy)
-        prepare_winh_piece(1, nc.vector.tensor_copy)
         for t in range(PACK):
             finish_direct(t)
-        for t in range(PACK):
+        sub_t[1] = held([P, PACK, P], F32, "sub_t1", "wsub_o")
+        finish_turned(1)
+        add(0)
+        prepare_winh_piece(1, nc.vector.tensor_copy, "inh00")
+        for t in range(1, PACK):
             add(t)
         for t in range(3):
             direct_root(t)
@@ -304,8 +305,10 @@ def tile_list_competitive_inhibitor_assay_kernel(
         direct_root(3)
         for pair in range(2):
             open_total(0, pair, pair)
-        for t in range(PACK):
+        for t in range(PACK - 1):
             scaled_product(left0[:, t, :], sub0[:, t, :], 0, t, root0[:, t, :])
+        for cols in (slice(0, HALF), slice(HALF, S)):
+            scaled_product(left0[:, 3, cols], sub0[:, 3, cols], 0, 3, root0[:, 3, cols])
         inhibitor_turned(1, 5)
         for pair in range(2):
             close_total(0, pair)
@@ -322,18 +325,18 @@ def tile_list_competitive_inhibitor_assay_kernel(
         h00 = quantize_rates("h00", h_bf00)
         inhibitor_turned(3, 4)
         turn_sub(1, 1, 7)
-        for pair in (1, 0):
+        for t in (2, 3):
+            left_on_scalar(1, t)
+        for pair in (0, 1):
             total_ps[1, pair] = bank(pair, [P, 2, HALF])
             for w in range(2):
                 turn_block(total_ps[1, pair], sub_t[2 + w], pair, w, w == 0, False)
                 turn_block(total_ps[1, pair], inh_t[2 + w], pair, w, False, w == 1)
         root = held([P, 2, HALF], F32, "root_last")
-        inverse_root(root[:], total_ps[1, 1][:])
         inverse_root(root1[1][:, pairs[0], :], total_ps[1, 0][:])
+        inverse_root(root[:], total_ps[1, 1][:])
         square(root1[1][:, pairs[1], :], root[:])
         turn_sub(1, 0, 2)
-        for t in (2, 3):
-            left_on_scalar(1, t)
         lefts(0, range(4))
         h01 = quantize_rates("h01", h_bf01)
         h_bf10 = rates("h_bf10", left1[0][:], root1[0][:])

@@ -349,21 +349,30 @@ def tile_list_competitive_inhibitor_assay_kernel(
             for c, h in enumerate((h00, h10)):
                 for e in range(2):
                     readout_pass(early[w][:, e, :], 2 * w + e, c, h, whole, c == 0 and e == 0, c == 1 and e == 1)
-            first = held([P, 2, HALF], F32, "first%d" % w)
-            nc.scalar.copy(first[:], early[w][:])
-            nc.sync.dma_start(out_rows[:, 2 * w : 2 * w + 2, :HALF], first[:])
-        late = [[bank(i, [P, 2, P]) for i in row] for row in ((6, 7), (0, 1))]
-        for u in range(2):
-            for n in range(4):
-                readout_pass(late[u][n // 2][:, n % 2, :], n, 0, h01, slice(u * P, (u + 1) * P), n % 2 == 0, False)
+            for e0, e1 in (((0, 1), (1, 2)), ((0, 2),))[w]:
+                first = held([P, e1 - e0, HALF], F32, "first%d%d" % (w, e0))
+                nc.scalar.copy(first[:], early[w][:, e0:e1, :])
+                nc.sync.dma_start(out_rows[:, 2 * w + e0 : 2 * w + e1, :HALF], first[:])
+        third = [bank(i, [P, 2, P]) for i in (6, 7)]
+        groups = ((0, 2), (2, 3), (3, 4))
+        last = [bank(i, [P, n1 - n0, P]) for i, (n0, n1) in enumerate(groups)]
+        for n in range(4):
+            readout_pass(third[n // 2][:, n % 2, :], n, 0, h01, slice(0, P), n % 2 == 0, False)
+        for i, (n0, n1) in enumerate(groups):
+            for n in range(n0, n1):
+                readout_pass(last[i][:, n - n0, :], n, 0, h01, slice(P, HALF), n == n0, False)
         h_late = [rates("h_bf11%d" % u, left1[1][:, :, u * P : (u + 1) * P], root1[1][:, :, u * P : (u + 1) * P])
                   for u in range(2)]
-        for u in range(2):
-            h = quantize_rates("h11%d" % u, h_late[u])
-            for n in range(4):
-                readout_pass(late[u][n // 2][:, n % 2, :], n, 1, h, slice(0, P), False, n % 2 == 1)
-            for w in range(2):
-                result = held([P, 2, P], F32, "last%d%d" % (u, w))
-                copy = nc.vector.tensor_copy if (u, w) == (1, 1) else nc.scalar.copy
-                copy(result[:], late[u][w][:])
-                nc.sync.dma_start(out_rows[:, 2 * w : 2 * w + 2, HALF + u * P : HALF + (u + 1) * P], result[:])
+        h11 = [quantize_rates("h11%d" % u, h_late[u]) for u in range(2)]
+        for n in range(4):
+            readout_pass(third[n // 2][:, n % 2, :], n, 1, h11[0], slice(0, P), False, n % 2 == 1)
+        for w in range(2):
+            result = held([P, 2, P], F32, "third%d" % w)
+            (nc.scalar.copy, nc.vector.tensor_copy)[w](result[:], third[w][:])
+            nc.sync.dma_start(out_rows[:, 2 * w : 2 * w + 2, HALF : HALF + P], result[:])
+        for i, (n0, n1) in enumerate(groups):
+            for n in range(n0, n1):
+                readout_pass(last[i][:, n - n0, :], n, 1, h11[1], slice(0, P), False, n == n1 - 1)
+            result = held([P, n1 - n0, P], F32, "last%d" % i)
+            (nc.scalar.copy, nc.vector.tensor_copy, nc.vector.tensor_copy)[i](result[:], last[i][:])
+            nc.sync.dma_start(out_rows[:, n0:n1, HALF + P :], result[:])

@@ -327,21 +327,31 @@ def tile_list_competitive_inhibitor_assay_kernel(
         turn_sub(1, 1, 7)
         for t in (2, 3):
             left_on_scalar(1, t)
-        for pair in (0, 1):
+        for pair in (1, 0):
             total_ps[1, pair] = bank(pair, [P, 2, HALF])
             for w in range(2):
                 turn_block(total_ps[1, pair], sub_t[2 + w], pair, w, w == 0, False)
                 turn_block(total_ps[1, pair], inh_t[2 + w], pair, w, False, w == 1)
         root = held([P, 2, HALF], F32, "root_last")
-        inverse_root(root1[1][:, pairs[0], :], total_ps[1, 0][:])
-        inverse_root(root[:], total_ps[1, 1][:])
-        square(root1[1][:, pairs[1], :], root[:])
+        blocks = (slice(0, P), slice(P, HALF))
+        for cols in blocks:
+            inverse_root(root[:, :, cols], total_ps[1, 1][:, :, cols])
+            inverse_root(root1[1][:, pairs[0], cols], total_ps[1, 0][:, :, cols])
+            square(root1[1][:, pairs[1], cols], root[:, :, cols])
         turn_sub(1, 0, 2)
         lefts(0, range(4))
         h01 = quantize_rates("h01", h_bf01)
         h_bf10 = rates("h_bf10", left1[0][:], root1[0][:])
-        lefts(1, range(2))
-        h10 = quantize_rates("h10", h_bf10)
+        h_late = []
+        for u, cols in enumerate(blocks):
+            for t in range(2):
+                scaled_product(left1[1][:, t, cols], sub_ps[1, 0][:, t, cols], 1, t, root1[1][:, t, cols])
+            if u == 0:
+                h10 = quantize_rates("h10", h_bf10)
+            else:
+                h11 = [quantize_rates("h110", h_late[0])]
+            h_late.append(rates("h_bf11%d" % u, left1[1][:, :, cols], root1[1][:, :, cols]))
+        h11.append(quantize_rates("h111", h_late[1]))
 
         out_rows = out.rearrange("(n p) j -> p n j", p=P)
         early = [bank(i, [P, 2, HALF]) for i in (5, 4)]
@@ -361,9 +371,6 @@ def tile_list_competitive_inhibitor_assay_kernel(
         for i, (n0, n1) in enumerate(groups):
             for n in range(n0, n1):
                 readout_pass(last[i][:, n - n0, :], n, 0, h01, slice(P, HALF), n == n0, False)
-        h_late = [rates("h_bf11%d" % u, left1[1][:, :, u * P : (u + 1) * P], root1[1][:, :, u * P : (u + 1) * P])
-                  for u in range(2)]
-        h11 = [quantize_rates("h11%d" % u, h_late[u]) for u in range(2)]
         for n in range(4):
             readout_pass(third[n // 2][:, n % 2, :], n, 1, h11[0], slice(0, P), False, n % 2 == 1)
         for w in range(2):

@@ -157,8 +157,8 @@ def tile_list_competitive_inhibitor_assay_kernel(
                 nc.tensor.matmul(dst[:, e, w * P : (w + 1) * P], blocks(e, w), identity[:],
                                  start=(start and i == 0), stop=(stop and i == 3), is_transpose=True)
 
-        def rates(name, left, right):
-            h_bf = held([P, left.shape[2], PACK], BF16, name)
+        def rates(name, left, right, home=None):
+            h_bf = held([P, left.shape[2], PACK], BF16, name, home)
             nc.vector.tensor_tensor(h_bf[:].rearrange("p (c i) t -> p c t i", i=4),
                                     left.rearrange("p t (c i) -> p c t i", i=4),
                                     right.rearrange("p t (c i) -> p c t i", i=4), ALU.mult)
@@ -321,7 +321,7 @@ def tile_list_competitive_inhibitor_assay_kernel(
         substrate_turned(turned_ps[3], 3, 0)
         finish_turned(3)
         h_bf00 = rates("h_bf00", left0[:, :, :HALF], root0[:, :, :HALF])
-        h_bf01 = rates("h_bf01", left0[:, :, HALF:], root0[:, :, HALF:])
+        h_bf02 = rates("h_bf02", left0[:, :, HALF : HALF + P], root0[:, :, HALF : HALF + P])
         h00 = quantize_rates("h00", h_bf00)
         inhibitor_turned(3, 4)
         turn_sub(1, 1, 7)
@@ -340,14 +340,16 @@ def tile_list_competitive_inhibitor_assay_kernel(
             square(root1[1][:, pairs[1], cols], root[:, :, cols])
         turn_sub(1, 0, 2)
         lefts(0, range(4))
-        h01 = quantize_rates("h01", h_bf01)
+        h02 = quantize_rates("h02", h_bf02)
         h_bf10 = rates("h_bf10", left1[0][:], root1[0][:])
+        h_bf03 = rates("h_bf03", left0[:, :, HALF + P :], root0[:, :, HALF + P :], "h_bf02")
+        h10 = quantize_rates("h10", h_bf10)
         h_late = []
         for u, cols in enumerate(blocks):
             for t in range(2):
                 scaled_product(left1[1][:, t, cols], sub_ps[1, 0][:, t, cols], 1, t, root1[1][:, t, cols])
             if u == 0:
-                h10 = quantize_rates("h10", h_bf10)
+                h03 = quantize_rates("h03", h_bf03)
             else:
                 h11 = [quantize_rates("h110", h_late[0])]
             h_late.append(rates("h_bf11%d" % u, left1[1][:, :, cols], root1[1][:, :, cols]))
@@ -367,10 +369,10 @@ def tile_list_competitive_inhibitor_assay_kernel(
         groups = ((0, 2), (2, 3), (3, 4))
         last = [bank(i, [P, n1 - n0, P]) for i, (n0, n1) in enumerate(groups)]
         for n in range(4):
-            readout_pass(third[n // 2][:, n % 2, :], n, 0, h01, slice(0, P), n % 2 == 0, False)
+            readout_pass(third[n // 2][:, n % 2, :], n, 0, h02, slice(0, P), n % 2 == 0, False)
         for i, (n0, n1) in enumerate(groups):
             for n in range(n0, n1):
-                readout_pass(last[i][:, n - n0, :], n, 0, h01, slice(P, HALF), n == n0, False)
+                readout_pass(last[i][:, n - n0, :], n, 0, h03, slice(0, P), n == n0, False)
         for n in range(4):
             readout_pass(third[n // 2][:, n % 2, :], n, 1, h11[0], slice(0, P), False, n % 2 == 1)
         for w in range(2):

@@ -72,7 +72,7 @@ def tile_list_competitive_inhibitor_assay_kernel(
 
         winh_rows = winh.rearrange("(p j) c -> p j c", j=PACK)
         rate = held([P, 2, PACK], F32, "rate")
-        wsub_w = held([P, 2, 2 * H], U8, "wsub_w")
+        wsub_w = [held([P, 2, 2 * PASS], U8, "wsub_w%d" % c) for c in range(2)]
         tab2_w = held([P, T2], I32, "tab2_w")
         tab_w = [held([P, T], I32, "tab_w%d" % g) for g in range(2)]
         wread_w = held([P, 2, N], I32, "wread_w")
@@ -86,6 +86,10 @@ def tile_list_competitive_inhibitor_assay_kernel(
 
         def load_tab(g, c0, c1):
             nc.sync.dma_start(tab_w[g][:, c0:c1], words(tab_words[g])[:, c0:c1])
+
+        def load_wsub(c):
+            nc.sync.dma_start(wsub_w[c][:].bitcast(I32),
+                              wsub_words.bitcast(I32).rearrange("g p c -> p g c")[:, :, c * HALF : (c + 1) * HALF])
 
         def close_ranks():
             for i in range(1, 4):
@@ -114,9 +118,9 @@ def tile_list_competitive_inhibitor_assay_kernel(
         nc.vector.tensor_copy(planes[:, :S].bitcast(I32), picked_sc[:].bitcast(I32))
         nc.vector.tensor_copy(v2_w[:], tab2_w[:].bitcast(U32).indirect(list2[:]))
         nc.vector.tensor_copy(v2_sc[:], tab2_sc[:, 0, :].indirect(list2[:]))
-        nc.sync.dma_start(wsub_w[:].bitcast(I32), wsub_words.bitcast(I32).rearrange("g p c -> p g c"))
-        move_second_pass(range(0, 2))
+        load_wsub(0)
         load_tab(0, 0, 1024)
+        move_second_pass(range(0, 2))
         close_ranks()
         load_tab(0, 1024, 2048)
         load_tab(1, 0, 1024)
@@ -124,6 +128,7 @@ def tile_list_competitive_inhibitor_assay_kernel(
         load_tab(1, 1024, 2048)
         load_winh(512, 256)
         load_winh(768, 256)
+        load_wsub(1)
         nc.sync.dma_start(rate[:], vmax.rearrange("(a p t) -> p a t", a=2, t=PACK))
         nc.sync.dma_start(wread_w[:], wread_words.rearrange("g p c i -> p g (c i)").bitcast(I32))
         load_scale_rows(wread_sc, wread_scales, WREAD_ROW, range(4))
@@ -136,7 +141,7 @@ def tile_list_competitive_inhibitor_assay_kernel(
         winh_sc = [held([P, PASS], U8, "winh_sc%d" % c) for c in range(2)]
         v_planes = (planes, planes_b)
 
-        sub_t = {q: held([P, PACK, P], F32, "sub_t%d" % q) for q in (0, 2, 3)}
+        sub_t = [held([P, PACK, P], F32, "sub_t%d" % q) for q in range(4)]
         inh_t = [held([P, PACK, P], F32, "inh_t%d" % q) for q in range(4)]
 
         def square(dst, src):
@@ -186,41 +191,38 @@ def tile_list_competitive_inhibitor_assay_kernel(
         nc.vector.quantize_mx(out=winh_w[0][:].bitcast(FP8X4), scales=winh_sc[0][:],
                               in_=winh_bf[:].rearrange("p t m j -> p (t m j)"))
         sub0, root0, left0 = [held([P, PACK, S], F32, name) for name in ("sub0", "root0", "left0")]
-        inh0 = [held([P, S], F32, "inh0%d" % t) for t in range(PACK)]
+        inh0 = held([P, PACK, S], F32, "inh0")
         for t in range(PACK):
             b_ps = bank(4 + t, [P, S])
             cols = slice(t * P, (t + 1) * P)
             nc.tensor.matmul_mx(out=b_ps[:], lhsT=winh_w[0][:, cols].bitcast(FP8X4), lhsT_scale=winh_sc[0][:, cols],
                                 rhs=v2_w[:].bitcast(FP8X4), rhs_scale=v2_sc[TAB2_ROW:P], start=True, stop=True)
-            square(inh0[t][:], b_ps[:])
+            square(inh0[:, t, :], b_ps[:])
 
         wsub_s = held([P, 2, PASS], U8, "wsub_s")
         nc.vector.tensor_copy(wsub_s[:].rearrange("p g (t m) -> p g t m", t=PACK),
                               planes[:, WSUB_AT:].rearrange("p (g c m t) -> p c g t m", g=2, c=2, t=PACK)[:, 0])
         wsub_o = held([P, 2, 2 * PASS], U8, "wsub_o")
         nc.vector.tensor_copy(wsub_o[:].bitcast(U16).rearrange("p g (t m) -> p g t m", t=PACK),
-                              wsub_w[:, :, : 2 * PASS].bitcast(U16).rearrange("p g (m t) -> p g t m", t=PACK))
+                              wsub_w[0][:].bitcast(U16).rearrange("p g (m t) -> p g t m", t=PACK))
 
-        def substrate_pass(a_ps, t, g):
-            nc.tensor.matmul_mx(out=a_ps[:], lhsT=wsub_o[:, g, 2 * t * P : 2 * (t + 1) * P].bitcast(FP4X4),
-                                lhsT_scale=wsub_s[:, g, t * P : (t + 1) * P],
-                                rhs=v_w[g][:].bitcast(FP8X4), rhs_scale=v_planes[g][:, :S],
-                                start=(g == 0), stop=(g == 1))
+        def substrate_direct(a_ps, u, pair, g):
+            for i, (e, w) in enumerate([(e, w) for e in range(2) for w in range(2)]):
+                t, cols = 2 * pair + e, slice((2 * u + w) * P, (2 * u + w + 1) * P)
+                nc.tensor.matmul_mx(out=a_ps[:, e, w * P : (w + 1) * P], lhsT=wsub_o[:, g, 2 * t * P : 2 * (t + 1) * P].bitcast(FP4X4),
+                                    lhsT_scale=wsub_s[:, g, t * P : (t + 1) * P],
+                                    rhs=v_w[g][:, cols].bitcast(FP8X4), rhs_scale=v_planes[g][:, cols],
+                                    start=(g == 0 and i == 0), stop=(g == 1 and i == 3))
 
-        def substrate_turned(a_ps, q, g):
-            first = WSUB_AT + g * H + PASS
-            nc.tensor.matmul_mx(out=a_ps[:], lhsT=v_w[g][:, q * P : (q + 1) * P].bitcast(FP8X4),
-                                lhsT_scale=v_planes[g][:, q * P : (q + 1) * P],
-                                rhs=wsub_w[:, g, 2 * PASS :].bitcast(FP4X4), rhs_scale=planes[:, first : first + PASS],
-                                start=(g == 0), stop=(g == 1))
-
-        def finish_turned(q):
-            substrate_turned(turned_ps[q], q, 1)
-            square(sub_t[q][:], turned_ps[q][:].rearrange("p (m t) -> p t m", t=PACK))
-
-        def finish_direct(t):
-            substrate_pass(a_ps[t], t, 1)
-            square(sub0[:, t, :], a_ps[t][:])
+        def substrate_turned(q, i):
+            a_ps = bank(i, [P, PASS])
+            for g in range(2):
+                first = WSUB_AT + g * H + PASS
+                nc.tensor.matmul_mx(out=a_ps[:], lhsT=v_w[g][:, q * P : (q + 1) * P].bitcast(FP8X4),
+                                    lhsT_scale=v_planes[g][:, q * P : (q + 1) * P],
+                                    rhs=wsub_w[1][:, g, :].bitcast(FP4X4), rhs_scale=planes[:, first : first + PASS],
+                                    start=(g == 0), stop=(g == 1))
+            square(sub_t[q][:], a_ps[:].rearrange("p (m t) -> p t m", t=PACK))
 
         def inhibitor_turned(q, i):
             b_ps = bank(i, [P, PASS])
@@ -237,7 +239,7 @@ def tile_list_competitive_inhibitor_assay_kernel(
             nc.vector.quantize_mx(out=winh_w[1][:, cols].bitcast(FP8X4), scales=winh_sc[1][:, cols],
                                   in_=grouped[:].rearrange("p c j -> p (c j)"))
 
-        root1, left1 = [[work("%s1%d" % (name, u)) for u in range(2)] for name in ("root", "left")]
+        root1, left1 = [[work(name + "10")[:], held([P, 2, PACK, P], F32, name + "11")] for name in ("root", "left")]
         total_ps, sub_ps = {}, {}
 
         def open_total(u, pair, i):
@@ -255,7 +257,8 @@ def tile_list_competitive_inhibitor_assay_kernel(
             square(root1[u][:, pairs[pair], :], root[:])
 
         def left_on_scalar(u, t):
-            nc.scalar.activation(left1[u][:, t, :], sub_ps[u, t // 2][:, t % 2, :], ACT.Copy, scale=rate[:, 1, t : t + 1])
+            nc.scalar.activation(left1[u][:, :, t, :], sub_ps[u, t // 2][:, t % 2, :].rearrange("p (w j) -> p w j", w=2),
+                                 ACT.Copy, scale=rate[:, 1, t : t + 1])
 
         def turn_block(dst, src, pair, w, start, stop):
             for e in range(2):
@@ -270,104 +273,103 @@ def tile_list_competitive_inhibitor_assay_kernel(
             for t in ts:
                 scaled_product(left1[u][:, t, :], sub_ps[u, t // 2][:, t % 2, :], 1, t, root1[u][:, t, :])
 
-        totals = {}
+        units = [(u, pair) for u in range(2) for pair in range(2)]
+        halves = (slice(0, HALF), slice(HALF, S))
 
-        def add(t, home=None):
-            totals[t] = held([P, S], F32, "total%d" % t, home)
-            nc.vector.tensor_tensor(totals[t][:], sub0[:, t, :], inh0[t][:], ALU.add)
+        def direct_root(u, pair):
+            total = held([P, 2, HALF], F32, "total%d%d" % (u, pair))
+            nc.vector.tensor_tensor(total[:], sub0[:, pairs[pair], halves[u]], inh0[:, pairs[pair], halves[u]], ALU.add)
+            inverse_root(root0[:, pairs[pair], halves[u]], total[:])
 
-        def direct_root(t):
-            inverse_root(root0[:, t, :], totals[t][:])
+        def direct_lefts(u):
+            for t in range(PACK):
+                scaled_product(left0[:, t, halves[u]], sub0[:, t, halves[u]], 0, t, root0[:, t, halves[u]])
 
         for u in range(2):
             gather_tab(0, u)
-        a_ps = [bank(t, [P, S]) for t in range(PACK)]
-        for t in range(PACK):
-            substrate_pass(a_ps[t], t, 0)
-        turned_ps = [bank(4 + q, [P, PASS]) for q in range(2)]
-        for q in range(2):
-            substrate_turned(turned_ps[q], q, 0)
+        a_ps = [bank(i, [P, 2, HALF]) for i in range(4)]
+        for i, (u, pair) in enumerate(units):
+            substrate_direct(a_ps[i], u, pair, 0)
         for u in range(2):
             gather_tab(1, u)
-        finish_turned(0)
+        for i, (u, pair) in enumerate(units):
+            substrate_direct(a_ps[i], u, pair, 1)
+            square(sub0[:, pairs[pair], halves[u]], a_ps[i][:])
+            if u == 0:
+                direct_root(u, pair)
+        for pair in range(2):
+            substrate_turned(pair, 4 - pair)
+            direct_root(1, pair)
         prepare_winh_piece(0, nc.vector.tensor_copy)
-        for t in range(PACK):
-            finish_direct(t)
-        sub_t[1] = held([P, PACK, P], F32, "sub_t1", "wsub_o")
-        finish_turned(1)
-        add(0)
-        prepare_winh_piece(1, nc.vector.tensor_copy, "inh00")
-        for t in range(1, PACK):
-            add(t)
-        for t in range(3):
-            direct_root(t)
-        inhibitor_turned(0, 4)
-        direct_root(3)
+        prepare_winh_piece(1, nc.vector.tensor_copy, "inh0")
+        direct_lefts(0)
+        direct_lefts(1)
+        inhibitor_turned(0, 6)
+        inhibitor_turned(1, 7)
         for pair in range(2):
             open_total(0, pair, pair)
-        for t in range(PACK - 1):
-            scaled_product(left0[:, t, :], sub0[:, t, :], 0, t, root0[:, t, :])
-        for cols in (slice(0, HALF), slice(HALF, S)):
-            scaled_product(left0[:, 3, cols], sub0[:, 3, cols], 0, 3, root0[:, 3, cols])
-        inhibitor_turned(1, 5)
         for pair in range(2):
             close_total(0, pair)
-            turn_sub(0, pair, (6, 3)[pair])
-        turned_ps.append(bank(2, [P, PASS]))
-        substrate_turned(turned_ps[2], 2, 0)
-        finish_turned(2)
-        inhibitor_turned(2, 4)
-        turned_ps.append(bank(5, [P, PASS]))
-        substrate_turned(turned_ps[3], 3, 0)
-        finish_turned(3)
+            turn_sub(0, pair, (2, 5)[pair])
+        substrate_turned(2, 4)
+        inhibitor_turned(2, 6)
+        substrate_turned(3, 3)
         h_bf00 = rates("h_bf00", left0[:, :, :HALF], root0[:, :, :HALF])
         h_bf02 = rates("h_bf02", left0[:, :, HALF : HALF + P], root0[:, :, HALF : HALF + P])
         h00 = quantize_rates("h00", h_bf00)
-        inhibitor_turned(3, 4)
-        turn_sub(1, 1, 7)
-        for t in (2, 3):
-            left_on_scalar(1, t)
-        for pair in (1, 0):
-            total_ps[1, pair] = bank(pair, [P, 2, HALF])
-            for w in range(2):
-                turn_block(total_ps[1, pair], sub_t[2 + w], pair, w, w == 0, False)
-                turn_block(total_ps[1, pair], inh_t[2 + w], pair, w, False, w == 1)
+        h_bf03 = rates("h_bf03", left0[:, :, HALF + P :], root0[:, :, HALF + P :])
+
+        def turn_all(dst, src, start, stop):
+            for t in range(PACK):
+                nc.tensor.matmul(dst[:, t, :], src[:, t, :], identity[:], start=(start and t == 0),
+                                 stop=(stop and t == PACK - 1), is_transpose=True)
+
+        def block_total(q, i):
+            total = bank(i, [P, PACK, P])
+            turn_all(total, sub_t[q], True, False)
+            turn_all(total, inh_t[q], False, True)
+            return total
+
+        def block_sub(q, i):
+            sub = bank(i, [P, PACK, P])
+            turn_all(sub, sub_t[q], True, True)
+            return sub
+
         root = held([P, 2, HALF], F32, "root_last")
-        blocks = (slice(0, P), slice(P, HALF))
-        for cols in blocks:
-            inverse_root(root[:, :, cols], total_ps[1, 1][:, :, cols])
-            inverse_root(root1[1][:, pairs[0], cols], total_ps[1, 0][:, :, cols])
-            square(root1[1][:, pairs[1], cols], root[:, :, cols])
-        turn_sub(1, 0, 2)
+        inverse_root(root1[1][:, 0], block_total(2, 4)[:])
+        sub2 = block_sub(2, 0)
+        inhibitor_turned(3, 7)
+        sub3 = block_sub(3, 1)
+        for t in range(PACK):
+            nc.scalar.activation(left1[1][:, 1, t, :], sub3[:, t, :], ACT.Copy, scale=rate[:, 1, t : t + 1])
+        inverse_root(root[:].rearrange("p e (w j) -> p (e w) j", w=2), block_total(3, 3)[:])
+        square(root1[1][:, 1], root[:].rearrange("p e (w j) -> p (e w) j", w=2))
         lefts(0, range(4))
         h02 = quantize_rates("h02", h_bf02)
-        h_bf10 = rates("h_bf10", left1[0][:], root1[0][:])
-        h_bf03 = rates("h_bf03", left0[:, :, HALF + P :], root0[:, :, HALF + P :], "h_bf02")
+        h_bf10 = rates("h_bf10", left1[0], root1[0])
+        h03 = quantize_rates("h03", h_bf03)
         h10 = quantize_rates("h10", h_bf10)
-        h_late = []
-        for u, cols in enumerate(blocks):
-            for t in range(2):
-                scaled_product(left1[1][:, t, cols], sub_ps[1, 0][:, t, cols], 1, t, root1[1][:, t, cols])
-            if u == 0:
-                h03 = quantize_rates("h03", h_bf03)
-            else:
-                h11 = [quantize_rates("h110", h_late[0])]
-            h_late.append(rates("h_bf11%d" % u, left1[1][:, :, cols], root1[1][:, :, cols]))
-        h11.append(quantize_rates("h111", h_late[1]))
+        for t in range(PACK):
+            scaled_product(left1[1][:, 0, t, :], sub2[:, t, :], 1, t, root1[1][:, 0, t, :])
+        h_late = [rates("h_bf11%d" % w, left1[1][:, w], root1[1][:, w]) for w in range(2)]
+        h11 = [quantize_rates("h11%d" % w, h_late[w]) for w in range(2)]
 
         out_rows = out.rearrange("(n p) j -> p n j", p=P)
-        early = [bank(i, [P, 2, HALF]) for i in (5, 4)]
+        early = [bank(i, [P, 2, HALF]) for i in (6, 4)]
         for w in range(2):
             for c, h in enumerate((h00, h10)):
                 for e in range(2):
                     readout_pass(early[w][:, e, :], 2 * w + e, c, h, whole, c == 0 and e == 0, c == 1 and e == 1)
             for e0, e1 in (((0, 1), (1, 2)), ((0, 2),))[w]:
-                first = held([P, e1 - e0, HALF], F32, "first%d%d" % (w, e0))
-                nc.scalar.copy(first[:], early[w][:, e0:e1, :])
-                nc.sync.dma_start(out_rows[:, 2 * w + e0 : 2 * w + e1, :HALF], first[:])
-        third = [bank(i, [P, 2, P]) for i in (6, 7)]
+                if w == 0:
+                    first = root[:, e0:e1]
+                else:
+                    first = held([P, 2, HALF], F32, "first1")[:]
+                nc.scalar.copy(first, early[w][:, e0:e1, :])
+                nc.sync.dma_start(out_rows[:, 2 * w + e0 : 2 * w + e1, :HALF], first)
+        third = [bank(i, [P, 2, P]) for i in (2, 5)]
         groups = ((0, 2), (2, 3), (3, 4))
-        last = [bank(i, [P, n1 - n0, P]) for i, (n0, n1) in enumerate(groups)]
+        last = [bank((0, 1, 7)[i], [P, n1 - n0, P]) for i, (n0, n1) in enumerate(groups)]
         for n in range(4):
             readout_pass(third[n // 2][:, n % 2, :], n, 0, h02, slice(0, P), n % 2 == 0, False)
         for i, (n0, n1) in enumerate(groups):

@@ -250,21 +250,6 @@ def tile_list_competitive_inhibitor_assay_kernel(
             turn(total_ps[u, pair], lambda e, w: inh_t[2 * u + w][:, 2 * pair + e, :], False, True)
             inverse_root(root1[u][:, pairs[pair], :], total_ps[u, pair][:])
 
-        def close_total_squared(u, pair):
-            turn(total_ps[u, pair], lambda e, w: inh_t[2 * u + w][:, 2 * pair + e, :], False, True)
-            root = held([P, 2, HALF], F32, "root_last")
-            inverse_root(root[:], total_ps[u, pair][:])
-            square(root1[u][:, pairs[pair], :], root[:])
-
-        def left_on_scalar(u, t):
-            nc.scalar.activation(left1[u][:, :, t, :], sub_ps[u, t // 2][:, t % 2, :].rearrange("p (w j) -> p w j", w=2),
-                                 ACT.Copy, scale=rate[:, 1, t : t + 1])
-
-        def turn_block(dst, src, pair, w, start, stop):
-            for e in range(2):
-                nc.tensor.matmul(dst[:, e, w * P : (w + 1) * P], src[:, 2 * pair + e, :], identity[:],
-                                 start=(start and e == 0), stop=(stop and e == 1), is_transpose=True)
-
         def turn_sub(u, pair, i):
             sub_ps[u, pair] = bank(i, [P, 2, HALF])
             turn(sub_ps[u, pair], lambda e, w: sub_t[2 * u + w][:, 2 * pair + e, :], True, True)
@@ -313,7 +298,7 @@ def tile_list_competitive_inhibitor_assay_kernel(
             turn_sub(0, pair, (2, 5)[pair])
         substrate_turned(2, 4)
         inhibitor_turned(2, 6)
-        substrate_turned(3, 3)
+        substrate_turned(3, 0)
         h_bf00 = rates("h_bf00", left0[:, :, :HALF], root0[:, :, :HALF])
         h_bf02 = rates("h_bf02", left0[:, :, HALF : HALF + P], root0[:, :, HALF : HALF + P])
         h00 = quantize_rates("h00", h_bf00)
@@ -337,12 +322,12 @@ def tile_list_competitive_inhibitor_assay_kernel(
 
         root = held([P, 2, HALF], F32, "root_last")
         inverse_root(root1[1][:, 0], block_total(2, 4)[:])
-        sub2 = block_sub(2, 0)
-        inhibitor_turned(3, 7)
-        sub3 = block_sub(3, 1)
+        sub2 = block_sub(2, 3)
+        inhibitor_turned(3, 1)
+        sub3 = block_sub(3, 7)
         for t in range(PACK):
             nc.scalar.activation(left1[1][:, 1, t, :], sub3[:, t, :], ACT.Copy, scale=rate[:, 1, t : t + 1])
-        inverse_root(root[:].rearrange("p e (w j) -> p (e w) j", w=2), block_total(3, 3)[:])
+        inverse_root(root[:].rearrange("p e (w j) -> p (e w) j", w=2), block_total(3, 0)[:])
         square(root1[1][:, 1], root[:].rearrange("p e (w j) -> p (e w) j", w=2))
         lefts(0, range(4))
         h02 = quantize_rates("h02", h_bf02)
@@ -369,7 +354,7 @@ def tile_list_competitive_inhibitor_assay_kernel(
                 nc.sync.dma_start(out_rows[:, 2 * w + e0 : 2 * w + e1, :HALF], first)
         third = [bank(i, [P, 2, P]) for i in (2, 5)]
         groups = ((0, 2), (2, 3), (3, 4))
-        last = [bank((0, 1, 7)[i], [P, n1 - n0, P]) for i, (n0, n1) in enumerate(groups)]
+        last = [bank((3, 7, 1)[i], [P, n1 - n0, P]) for i, (n0, n1) in enumerate(groups)]
         for n in range(4):
             readout_pass(third[n // 2][:, n % 2, :], n, 0, h02, slice(0, P), n % 2 == 0, False)
         for i, (n0, n1) in enumerate(groups):

from contextlib import ExitStack

import concourse.mybir as mybir
from concourse.masks import make_identity

K, K2, H, N, T, T2, S = 1024, 512, 1024, 512, 2048, 1024, 512
FLOPS = 2 * S * (K * H + K2 * H + H * N)

F32 = mybir.dt.float32
BF16 = mybir.dt.bfloat16
I32 = mybir.dt.int32
U32 = mybir.dt.uint32
U16 = mybir.dt.uint16
U8 = mybir.dt.uint8
FP8X4 = mybir.dt.float8_e4m3fn_x4
FP4X4 = mybir.dt.float4_e2m1fn_x4
ACT = mybir.ActivationFunctionType
ALU = mybir.AluOpType

P = 128
PACK = 4
PASS = P * PACK
HALF = S // 2
WSUB_AT = S
PLANE_BYTES = WSUB_AT + 2 * H
TAB2_ROW = 4
WREAD_ROW = 8


def tile_list_competitive_inhibitor_assay_kernel(
    tc, tab_words, tab_scales, offs, tab2_words, tab2_scales, offs2,
    wsub_words, wsub_scales, winh, vmax, wread_words, wread_scales, out,
):
    nc = tc.nc
    with ExitStack() as ctx:
        keep = ctx.enter_context(tc.tile_pool(name="keep", bufs=1))
        psum = ctx.enter_context(tc.psum_pool(name="psum", bufs=1))

        def bank(i, shape):
            return psum.tile(shape, F32, name="bank%d" % i)

        def held(shape, dtype, name, tag=None):
            return keep.tile(shape, dtype, name=name, tag=tag or name, align_bytes=64)

        lists = keep.tile([P, S // 16], U16, name="lists")
        list2 = keep.tile([P, S // 16], U16, name="list2")

        seed = held([P, 1], F32, "seed")
        one = held([P, 1], F32, "one")
        identity = held([P, P], F32, "identity")

        tab_sc = held([P, T], U8, "tab_sc")
        tab2_sc = held([P, 1, T2], U8, "tab2_sc")
        wread_sc = held([P, 2, N], U8, "wread_sc")
        planes = held([P, PLANE_BYTES], U8, "planes")
        planes_b = held([P, S], U8, "planes_b")
        nc.vector.memset(tab_sc[:].bitcast(I32), 0)
        nc.vector.memset(tab2_sc[:].bitcast(I32), 0)
        nc.vector.memset(seed[:], 1.0)
        nc.vector.memset(planes[:, WSUB_AT:].bitcast(I32), 0)
        nc.vector.memset(planes_b[:].bitcast(I32), 0)
        nc.vector.memset(wread_sc[:].bitcast(I32), 0)
        nc.vector.memset(identity[:], 0.0)
        nc.scalar.activation(one[:], seed[:], ACT.Abs_reciprocal_sqrt)
        make_identity(nc, identity[:], nomemset=True)

        def words(src):
            return src.rearrange("p t i -> p (t i)").bitcast(I32)

        def scale_rows(src):
            return src.bitcast(I32).rearrange("a q c -> q a c")

        winh_rows = winh.rearrange("(p j) c -> p j c", j=PACK)
        rate = held([P, 2, PACK], F32, "rate")
        wsub_w = [held([P, 2, 2 * PASS], U8, "wsub_w%d" % c) for c in range(2)]
        tab2_w = held([P, T2], I32, "tab2_w")
        tab_w = [held([P, T], I32, "tab_w%d" % g) for g in range(2)]
        wread_w = held([P, 2, N], I32, "wread_w")
        picked_sc = held([P, S], U8, "picked_sc")
        v2_sc = held([P, S], U8, "v2_sc")
        winh_raw = {}

        def load_winh(c0, width):
            winh_raw[c0] = held([P, PACK, width], F32, "winh_raw%d" % c0)
            nc.sync.dma_start(winh_raw[c0][:], winh_rows[:, :, c0 : c0 + width])

        def load_tab(g, c0, c1):
            nc.sync.dma_start(tab_w[g][:, c0:c1], words(tab_words[g])[:, c0:c1])

        def load_wsub(c):
            nc.sync.dma_start(wsub_w[c][:].bitcast(I32),
                              wsub_words.bitcast(I32).rearrange("g p c -> p g c")[:, :, c * HALF : (c + 1) * HALF])

        def close_ranks():
            for i in range(1, 4):
                nc.sync.dma_start(planes[i:P:32].bitcast(I32), planes[8 * i : P : 32].bitcast(I32))

        def move_second_pass(rows):
            for i in rows:
                nc.sync.dma_start(planes_b[i:P:32].bitcast(I32), picked_sc[8 * i + 4 : P : 32].bitcast(I32))

        v_w = [held([P, S], U32, "v_w%d" % g) for g in range(2)]
        v2_w = held([P, S], U32, "v2_w")

        def load_scale_rows(dst, src, first, rows):
            for r in rows:
                nc.sync.dma_start(dst[:].bitcast(I32)[first + r : P : 32], scale_rows(src)[r:16:4])

        nc.sync.dma_start(tab2_w[:], words(tab2_words[0]))
        nc.sync.dma_start(lists[:], offs)
        nc.sync.dma_start(tab_sc[0:P:4].bitcast(I32), scale_rows(tab_scales))
        nc.sync.dma_start(list2[:], offs2)
        load_scale_rows(tab2_sc, tab2_scales, TAB2_ROW, range(0, 2))
        load_winh(0, PASS)
        load_scale_rows(tab2_sc, tab2_scales, TAB2_ROW, range(2, 4))
        nc.sync.dma_start(planes[0:P:8, WSUB_AT:].bitcast(I32).rearrange("q (a c) -> q a c", a=2), scale_rows(wsub_scales))
        nc.vector.tensor_copy(picked_sc[:], tab_sc[:].indirect(lists[:]))
        nc.vector.tensor_copy(planes[:, :S].bitcast(I32), picked_sc[:].bitcast(I32))
        nc.vector.tensor_copy(v2_w[:], tab2_w[:].bitcast(U32).indirect(list2[:]))
        nc.vector.tensor_copy(v2_sc[:], tab2_sc[:, 0, :].indirect(list2[:]))
        load_wsub(0)
        load_tab(0, 0, 1024)
        move_second_pass(range(0, 2))
        close_ranks()
        load_tab(0, 1024, 2048)
        load_tab(1, 0, 1024)
        move_second_pass(range(2, 4))
        load_tab(1, 1024, 2048)
        load_winh(512, 256)
        load_winh(768, 256)
        load_wsub(1)
        nc.sync.dma_start(rate[:], vmax.rearrange("(a p t) -> p a t", a=2, t=PACK))
        nc.sync.dma_start(wread_w[:], wread_words.rearrange("g p c i -> p g (c i)").bitcast(I32))
        load_scale_rows(wread_sc, wread_scales, WREAD_ROW, range(4))

        def gather_tab(g, u):
            nc.vector.tensor_copy(v_w[g][:, u * HALF : (u + 1) * HALF],
                                  tab_w[g][:].bitcast(U32).indirect(lists[:, 16 * u : 16 * (u + 1)]))

        winh_w = [held([P, PASS], U32, "winh_w%d" % c) for c in range(2)]
        winh_sc = [held([P, PASS], U8, "winh_sc%d" % c) for c in range(2)]
        v_planes = (planes, planes_b)

        sub_t = [held([P, PACK, P], F32, "sub_t%d" % q) for q in range(4)]
        inh_t = [held([P, PACK, P], F32, "inh_t%d" % q) for q in range(4)]

        def square(dst, src):
            nc.scalar.activation(dst, src, ACT.Square)

        def inverse_root(dst, total):
            nc.scalar.activation(dst, total, ACT.Abs_reciprocal_sqrt, bias=one[:])

        def scaled_product(dst, sub, c, t, root):
            nc.vector.scalar_tensor_tensor(dst, sub, rate[:, c, t : t + 1], root, ALU.mult, ALU.mult)

        def work(name):
            return held([P, PACK, HALF], F32, name)

        def turn(dst, blocks, start, stop):
            steps = [(e, w) for w in range(2) for e in range(2)]
            for i, (e, w) in enumerate(steps):
                nc.tensor.matmul(dst[:, e, w * P : (w + 1) * P], blocks(e, w), identity[:],
                                 start=(start and i == 0), stop=(stop and i == 3), is_transpose=True)

        def rates(name, left, right, home=None):
            h_bf = held([P, left.shape[2], PACK], BF16, name, home)
            nc.vector.tensor_tensor(h_bf[:].rearrange("p (c i) t -> p c t i", i=4),
                                    left.rearrange("p t (c i) -> p c t i", i=4),
                                    right.rearrange("p t (c i) -> p c t i", i=4), ALU.mult)
            return h_bf

        def quantize_rates(name, h_bf):
            codes = held([P, h_bf.shape[1]], U32, name + "_w")
            scales = held([P, h_bf.shape[1]], U8, name + "_sc")
            nc.vector.quantize_mx(out=codes[:].bitcast(FP8X4), scales=scales[:],
                                  in_=h_bf[:].rearrange("p j t -> p (j t)"))
            return codes, scales

        def readout_pass(o_ps, n, c, h, cols, start, stop):
            nc.tensor.matmul_mx(out=o_ps, lhsT=wread_w[:, c, n * P : (n + 1) * P].bitcast(FP8X4),
                                lhsT_scale=wread_sc[WREAD_ROW:P, c, n * P : (n + 1) * P], rhs=h[0][:, cols].bitcast(FP8X4),
                                rhs_scale=h[1][:, cols], start=start, stop=stop)

        whole = slice(0, HALF)
        pairs = (slice(0, 2), slice(2, 4))

        winh_bf = held([P, PACK, P, PACK], BF16, "winh_bf0")
        for piece in range(2):
            nc.scalar.copy(winh_bf[:, :, piece * P // 2 : (piece + 1) * P // 2, :].rearrange("p t m j -> p m j t"),
                           winh_raw[0][:, :, piece * HALF : (piece + 1) * HALF].rearrange("p j (m t) -> p m j t", t=PACK))
        nc.vector.quantize_mx(out=winh_w[0][:].bitcast(FP8X4), scales=winh_sc[0][:],
                              in_=winh_bf[:].rearrange("p t m j -> p (t m j)"))
        sub0, root0, left0 = [held([P, PACK, S], F32, name) for name in ("sub0", "root0", "left0")]
        inh0 = held([P, PACK, S], F32, "inh0")
        for t in range(PACK):
            b_ps = bank(4 + t, [P, S])
            cols = slice(t * P, (t + 1) * P)
            nc.tensor.matmul_mx(out=b_ps[:], lhsT=winh_w[0][:, cols].bitcast(FP8X4), lhsT_scale=winh_sc[0][:, cols],
                                rhs=v2_w[:].bitcast(FP8X4), rhs_scale=v2_sc[TAB2_ROW:P], start=True, stop=True)
            square(inh0[:, t, :], b_ps[:])

        wsub_s = held([P, 2, PASS], U8, "wsub_s")
        nc.vector.tensor_copy(wsub_s[:].rearrange("p g (t m) -> p g t m", t=PACK),
                              planes[:, WSUB_AT:].rearrange("p (g c m t) -> p c g t m", g=2, c=2, t=PACK)[:, 0])
        wsub_o = held([P, 2, 2 * PASS], U8, "wsub_o")
        nc.vector.tensor_copy(wsub_o[:].bitcast(U16).rearrange("p g (t m) -> p g t m", t=PACK),
                              wsub_w[0][:].bitcast(U16).rearrange("p g (m t) -> p g t m", t=PACK))

        def substrate_direct(a_ps, u, pair, g):
            for i, (e, w) in enumerate([(e, w) for e in range(2) for w in range(2)]):
                t, cols = 2 * pair + e, slice((2 * u + w) * P, (2 * u + w + 1) * P)
                nc.tensor.matmul_mx(out=a_ps[:, e, w * P : (w + 1) * P], lhsT=wsub_o[:, g, 2 * t * P : 2 * (t + 1) * P].bitcast(FP4X4),
                                    lhsT_scale=wsub_s[:, g, t * P : (t + 1) * P],
                                    rhs=v_w[g][:, cols].bitcast(FP8X4), rhs_scale=v_planes[g][:, cols],
                                    start=(g == 0 and i == 0), stop=(g == 1 and i == 3))

        def substrate_turned(q, i):
            a_ps = bank(i, [P, PASS])
            for g in range(2):
                first = WSUB_AT + g * H + PASS
                nc.tensor.matmul_mx(out=a_ps[:], lhsT=v_w[g][:, q * P : (q + 1) * P].bitcast(FP8X4),
                                    lhsT_scale=v_planes[g][:, q * P : (q + 1) * P],
                                    rhs=wsub_w[1][:, g, :].bitcast(FP4X4), rhs_scale=planes[:, first : first + PASS],
                                    start=(g == 0), stop=(g == 1))
            square(sub_t[q][:], a_ps[:].rearrange("p (m t) -> p t m", t=PACK))

        def inhibitor_turned(q, i):
            b_ps = bank(i, [P, PASS])
            nc.tensor.matmul_mx(out=b_ps[:], lhsT=v2_w[:, q * P : (q + 1) * P].bitcast(FP8X4),
                                lhsT_scale=v2_sc[TAB2_ROW:P, q * P : (q + 1) * P],
                                rhs=winh_w[1][:].bitcast(FP8X4), rhs_scale=winh_sc[1][:], start=True, stop=True)
            square(inh_t[q][:], b_ps[:].rearrange("p (m t) -> p t m", t=PACK))

        def prepare_winh_piece(piece, copy, home=None):
            cols = slice(piece * HALF, (piece + 1) * HALF)
            grouped = held([P, HALF, PACK], BF16, "winh_bf1%d" % piece, home)
            copy(grouped[:].rearrange("p (c i) j -> p c j i", i=4),
                 winh_raw[PASS + cols.start][:].rearrange("p j (c i) -> p c j i", i=4))
            nc.vector.quantize_mx(out=winh_w[1][:, cols].bitcast(FP8X4), scales=winh_sc[1][:, cols],
                                  in_=grouped[:].rearrange("p c j -> p (c j)"))

        root1, left1 = [[work(name + "10")[:], held([P, 2, PACK, P], F32, name + "11")] for name in ("root", "left")]
        total_ps, sub_ps = {}, {}

        def open_total(u, pair, i):
            total_ps[u, pair] = bank(i, [P, 2, HALF])
            turn(total_ps[u, pair], lambda e, w: sub_t[2 * u + w][:, 2 * pair + e, :], True, False)

        def close_total(u, pair):
            turn(total_ps[u, pair], lambda e, w: inh_t[2 * u + w][:, 2 * pair + e, :], False, True)
            inverse_root(root1[u][:, pairs[pair], :], total_ps[u, pair][:])

        def turn_sub(u, pair, i):
            sub_ps[u, pair] = bank(i, [P, 2, HALF])
            turn(sub_ps[u, pair], lambda e, w: sub_t[2 * u + w][:, 2 * pair + e, :], True, True)

        def lefts(u, ts):
            for t in ts:
                scaled_product(left1[u][:, t, :], sub_ps[u, t // 2][:, t % 2, :], 1, t, root1[u][:, t, :])

        units = [(u, pair) for u in range(2) for pair in range(2)]
        halves = (slice(0, HALF), slice(HALF, S))

        def direct_root(u, pair):
            total = held([P, 2, HALF], F32, "total%d%d" % (u, pair))
            nc.vector.tensor_tensor(total[:], sub0[:, pairs[pair], halves[u]], inh0[:, pairs[pair], halves[u]], ALU.add)
            inverse_root(root0[:, pairs[pair], halves[u]], total[:])

        def direct_lefts(u):
            for t in range(PACK):
                scaled_product(left0[:, t, halves[u]], sub0[:, t, halves[u]], 0, t, root0[:, t, halves[u]])

        for u in range(2):
            gather_tab(0, u)
        a_ps = [bank(i, [P, 2, HALF]) for i in range(4)]
        for i, (u, pair) in enumerate(units):
            substrate_direct(a_ps[i], u, pair, 0)
        for u in range(2):
            gather_tab(1, u)
        for i, (u, pair) in enumerate(units):
            substrate_direct(a_ps[i], u, pair, 1)
            square(sub0[:, pairs[pair], halves[u]], a_ps[i][:])
            if u == 0:
                direct_root(u, pair)
        for pair in range(2):
            substrate_turned(pair, 4 - pair)
            direct_root(1, pair)
        prepare_winh_piece(0, nc.vector.tensor_copy)
        prepare_winh_piece(1, nc.vector.tensor_copy, "inh0")
        direct_lefts(0)
        direct_lefts(1)
        inhibitor_turned(0, 6)
        inhibitor_turned(1, 7)
        for pair in range(2):
            open_total(0, pair, pair)
        for pair in range(2):
            close_total(0, pair)
            turn_sub(0, pair, (2, 5)[pair])
        substrate_turned(2, 4)
        inhibitor_turned(2, 6)
        substrate_turned(3, 0)
        h_bf00 = rates("h_bf00", left0[:, :, :HALF], root0[:, :, :HALF])
        h_bf02 = rates("h_bf02", left0[:, :, HALF : HALF + P], root0[:, :, HALF : HALF + P])
        h00 = quantize_rates("h00", h_bf00)
        h_bf03 = rates("h_bf03", left0[:, :, HALF + P :], root0[:, :, HALF + P :])

        def turn_all(dst, src, start, stop):
            for t in range(PACK):
                nc.tensor.matmul(dst[:, t, :], src[:, t, :], identity[:], start=(start and t == 0),
                                 stop=(stop and t == PACK - 1), is_transpose=True)

        def block_total(q, i):
            total = bank(i, [P, PACK, P])
            turn_all(total, sub_t[q], True, False)
            turn_all(total, inh_t[q], False, True)
            return total

        def block_sub(q, i):
            sub = bank(i, [P, PACK, P])
            turn_all(sub, sub_t[q], True, True)
            return sub

        root = held([P, 2, HALF], F32, "root_last")
        inverse_root(root1[1][:, 0], block_total(2, 4)[:])
        sub2 = block_sub(2, 3)
        inhibitor_turned(3, 1)
        sub3 = block_sub(3, 7)
        for t in range(PACK):
            nc.scalar.activation(left1[1][:, 1, t, :], sub3[:, t, :], ACT.Copy, scale=rate[:, 1, t : t + 1])
        inverse_root(root[:].rearrange("p e (w j) -> p (e w) j", w=2), block_total(3, 0)[:])
        square(root1[1][:, 1], root[:].rearrange("p e (w j) -> p (e w) j", w=2))
        lefts(0, range(4))
        h02 = quantize_rates("h02", h_bf02)
        h_bf10 = rates("h_bf10", left1[0], root1[0])
        h03 = quantize_rates("h03", h_bf03)
        h10 = quantize_rates("h10", h_bf10)
        for t in range(PACK):
            scaled_product(left1[1][:, 0, t, :], sub2[:, t, :], 1, t, root1[1][:, 0, t, :])
        h_late = [rates("h_bf11%d" % w, left1[1][:, w], root1[1][:, w]) for w in range(2)]
        h11 = [quantize_rates("h11%d" % w, h_late[w]) for w in range(2)]

        out_rows = out.rearrange("(n p) j -> p n j", p=P)
        early = [bank(i, [P, 2, HALF]) for i in (6, 4)]
        for w in range(2):
            for c, h in enumerate((h00, h10)):
                for e in range(2):
                    readout_pass(early[w][:, e, :], 2 * w + e, c, h, whole, c == 0 and e == 0, c == 1 and e == 1)
            for e0, e1 in (((0, 1), (1, 2)), ((0, 2),))[w]:
                if w == 0:
                    first = root[:, e0:e1]
                else:
                    first = held([P, 2, HALF], F32, "first1")[:]
                nc.scalar.copy(first, early[w][:, e0:e1, :])
                nc.sync.dma_start(out_rows[:, 2 * w + e0 : 2 * w + e1, :HALF], first)
        third = [bank(i, [P, 2, P]) for i in (2, 5)]
        groups = ((0, 2), (2, 3), (3, 4))
        last = [bank((3, 7, 1)[i], [P, n1 - n0, P]) for i, (n0, n1) in enumerate(groups)]
        for n in range(4):
            readout_pass(third[n // 2][:, n % 2, :], n, 0, h02, slice(0, P), n % 2 == 0, False)
        for i, (n0, n1) in enumerate(groups):
            for n in range(n0, n1):
                readout_pass(last[i][:, n - n0, :], n, 0, h03, slice(0, P), n == n0, False)
        for n in range(4):
            readout_pass(third[n // 2][:, n % 2, :], n, 1, h11[0], slice(0, P), False, n % 2 == 1)
        for w in range(2):
            result = held([P, 2, P], F32, "third%d" % w)
            (nc.scalar.copy, nc.vector.tensor_copy)[w](result[:], third[w][:])
            nc.sync.dma_start(out_rows[:, 2 * w : 2 * w + 2, HALF : HALF + P], result[:])
        for i, (n0, n1) in enumerate(groups):
            for n in range(n0, n1):
                readout_pass(last[i][:, n - n0, :], n, 1, h11[1], slice(0, P), False, n == n1 - 1)
            result = held([P, n1 - n0, P], F32, "last%d" % i)
            (nc.scalar.copy, nc.vector.tensor_copy, nc.vector.tensor_copy)[i](result[:], last[i][:])
            nc.sync.dma_start(out_rows[:, n0:n1, HALF + P :], result[:])
